import numpy as np
import ml_dtypes


def mxq(x, axis, fmt="e4m3"):
    dtype, down = {"e4m3": (ml_dtypes.float8_e4m3fn, 7), "e5m2": (ml_dtypes.float8_e5m2, 14)}[fmt]
    v = np.moveaxis(np.asarray(x, np.float32).astype(ml_dtypes.bfloat16).astype(np.float64), axis, -1)
    blocks = v.reshape(v.shape[:-1] + (-1, 32))
    amax = np.abs(blocks).max(-1, keepdims=True)
    byte = np.maximum(np.where(amax > 0, np.frexp(amax)[1] - 1 + 127, 0) - down, 1)
    scale = np.exp2(byte - 127.0)
    codes = (blocks / scale).astype(np.float32).astype(dtype).astype(np.float64)
    return np.moveaxis((codes * scale).reshape(v.shape), -1, axis)


WIDE = False


def mx_kscale(k):
    if not WIDE:
        return np.ones(k)
    levels = np.array([10, -10, 5, -5, 0])
    if k % 512:
        return np.exp2(np.random.permutation(np.resize(levels, k // 32))).repeat(32)
    a = np.empty((k // 512, 16))
    for p in range(k // 512):
        a[p, :8] = np.random.permutation(np.resize(levels, 8))
        for g in range(8):
            far = levels[np.abs(levels - a[p, g]) >= 10]
            a[p, g + 8] = far[np.random.randint(len(far))]
    return np.exp2(a.ravel()).repeat(32)


def f64(x):
    return np.asarray(x).astype(np.float64)


def striped(idx):
    return np.tile(idx.reshape(-1, 16).T, (8, 1)).astype(np.uint16)


def unstriped(offs):
    return offs[:16].T.reshape(-1).astype(np.int64)


def striped8(idx):
    return np.concatenate([x.reshape(-1, 16).T for x in idx]).astype(np.uint16)


def runs(offs, k):
    lists = np.stack([offs[16 * r : 16 * r + 16].T.reshape(-1) for r in range(8)]).astype(np.int64)
    return lists[np.arange(k) % 512 // 64]


def pack_weight(w):
    k, n = w.shape
    w = f64(np.asarray(w, np.float32).astype(ml_dtypes.bfloat16)).reshape(k // 32, 32, n)
    amax = np.abs(w).max(1)
    byte = np.clip(np.where(amax > 0, np.frexp(amax)[1] - 1 + 127 - 7, 1), 1, 254)
    scaled = (w * np.exp2(127.0 - byte)[:, None, :]).reshape(k, n).astype(np.float32)
    words = np.ascontiguousarray(scaled.reshape(k // 512, 128, 4, n).transpose(0, 1, 3, 2)).astype(ml_dtypes.float8_e4m3fn).view(np.uint8)
    return words, np.ascontiguousarray(byte.astype(np.uint8).reshape(k // 512, 16, n))


def unpack_weight(words, scales):
    g, p, n, _ = words.shape
    vals = np.ascontiguousarray(words).view(ml_dtypes.float8_e4m3fn).astype(np.float64) * np.repeat(np.exp2(scales.astype(np.float64) - 127.0), 8, axis=1)[..., None]
    return vals.transpose(0, 1, 3, 2).reshape(g * 512, n)

def planes(y):
    n, m = y.shape
    v = y.astype(np.float32).astype(ml_dtypes.bfloat16).astype(np.float64).reshape(n // 32, 32, m)
    top = np.abs(v).max(1)
    byte = np.clip(np.where(top > 0, np.frexp(top)[1] - 1 + 127 - 7, 1), 1, 254)
    codes = (v * np.exp2(127.0 - byte)[:, None, :]).reshape(n, m).astype(np.float32).astype(ml_dtypes.float8_e4m3fn).view(np.uint8)
    words = codes.reshape(n // 512, 128, 4, m).transpose(0, 1, 3, 2)
    return np.ascontiguousarray(words), np.ascontiguousarray(byte.astype(np.uint8).reshape(n // 512, 16, m))


K, T, S, N, G, H = 512, 1024, 512, 512, 2048, 512


def setup_inputs():
    n = np.random.standard_normal
    s = mx_kscale(K)[:, None]
    u = mx_kscale(S)
    packed_xT = pack_weight(n((K, T)) * s)
    packed_dT = pack_weight(n((K, G)) / s)
    packed_w1 = pack_weight(n((H, N)) / np.sqrt(2 * H) / u[:, None])
    packed_w2 = pack_weight(n((H, N)) / np.sqrt(2 * H) / u[:, None])
    return {
        "x_words": packed_xT[0],
        "x_scales": packed_xT[1],
        "d_words": packed_dT[0],
        "d_scales": packed_dT[1],
        "gn": (np.random.uniform(0.5, 1.5, (H, 1)) * u[:, None]).astype(np.float32),
        "gm": (np.random.uniform(0.5, 1.5, (H, 1)) * u[:, None]).astype(np.float32),
        "w1_words": packed_w1[0],
        "w1_scales": packed_w1[1],
        "w2_words": packed_w2[0],
        "w2_scales": packed_w2[1],
        "offs": striped(np.random.permutation(T)[:S]),
        "k1": striped8(np.random.randint(0, G, (8, H))),
        "two": striped(np.random.permutation(T)[:S]),
        "n1": striped8(np.stack([np.random.permutation(S) for _ in range(8)])),
        "n2": striped8(np.stack([np.random.permutation(S) for _ in range(8)])),
        "n3": striped8(np.stack([np.random.permutation(S) for _ in range(8)])),
        "n4": striped8(np.stack([np.random.permutation(S) for _ in range(8)])),
        "n5": striped(np.random.randint(0, S, G)),
    }


def reference(x_words, x_scales, d_words, d_scales, gn, gm, w1_words, w1_scales, w2_words, w2_scales, offs, k1, two, n1, n2, n3, n4, n5):
    d_k1 = unpack_weight(d_words, d_scales)[np.arange(K)[:, None], runs(k1, K)]
    xq = unpack_weight(x_words, x_scales)[:, unstriped(offs)]
    a = 0.0625 * (d_k1.T @ xq)
    z = f64(gn) * (a[np.arange(H)[:, None], runs(n1, H)] - (a[np.arange(H)[:, None], runs(n2, H)]))
    x_two = unpack_weight(x_words, x_scales)[:, unstriped(two)]
    b = 0.0625 * (d_k1.T @ x_two)
    ex = np.exp(b)
    z2 = f64(gm) * (np.log(ex + ex[np.arange(H)[:, None], runs(n3, H)]) - (b[np.arange(H)[:, None], runs(n4, H)]))
    h = unpack_weight(w1_words, w1_scales).T @ mxq(z, 0, "e4m3") + unpack_weight(w2_words, w2_scales).T @ mxq(z2, 0, "e4m3")
    mb = h[:, unstriped(n5)]
    mx = mb.reshape(N, S, 4).max(axis=2)
    mn = mb.reshape(N, S, 4).min(axis=2)
    out_0 = mx - (0.5 * mn)
    return (out_0,) + planes(out_0)

@@ -1,0 +1,237 @@
+from contextlib import ExitStack
+
+import concourse.mybir as mybir
+from concourse.masks import make_identity
+
+F32 = mybir.dt.float32
+BF16 = mybir.dt.bfloat16
+I32 = mybir.dt.int32
+U32 = mybir.dt.uint32
+U16 = mybir.dt.uint16
+U8 = mybir.dt.uint8
+FP8X4 = mybir.dt.float8_e4m3fn_x4
+ALU = mybir.AluOpType
+ACT = mybir.ActivationFunctionType
+
+P = 128
+PACK = 4
+K, T, S, N, G, H = 512, 1024, 512, 512, 2048, 512
+HALF = S // 2
+CHUNK = 512
+SPARE = 16
+FLOPS = 4 * 2 * 512 * 512 * 512
+
+
+def tile_picked_kjgaplsegspan_none_po_kernel(tc, x_words, x_scales, d_words, d_scales, gn, gm, w1_words, w1_scales, w2_words, w2_scales, offs, k1, two, n1, n2, n3, n4, n5, out_0, out_1, out_2):
+    nc = tc.nc
+
+    def words_of(dram):
+        return dram[0].rearrange("p c r -> p (c r)").bitcast(I32)
+
+    def deal(dst, src):
+        nc.vector.tensor_copy(out=dst.rearrange("p (t m) -> p t m", t=PACK), in_=src.rearrange("p (m t) -> p t m", t=PACK))
+
+    def interleave(dst, src):
+        nc.vector.tensor_copy(out=dst.rearrange("p (c i t) -> p c t i", i=4, t=PACK), in_=src.rearrange("p t (c i) -> p c t i", i=4))
+
+    with ExitStack() as ctx:
+        lists = ctx.enter_context(tc.tile_pool(name="lists", bufs=1))
+        keep = ctx.enter_context(tc.tile_pool(name="keep", bufs=1))
+        ring = ctx.enter_context(tc.tile_pool(name="ring", bufs=3))
+        psum = ctx.enter_context(tc.psum_pool(name="psum", bufs=1))
+
+        def load_list(dram, name):
+            tile = lists.tile(list(dram.shape), U16, name=name)
+            nc.sync.dma_start(tile[:], dram)
+            return tile
+
+        d_bytes = keep.tile([P, G], U8, name="d_bytes", align_bytes=64)
+        x_bytes = keep.tile([P, T], U8, name="x_bytes", align_bytes=64)
+        key_scales = keep.tile([P, H], U8, name="key_scales", align_bytes=64)
+        nc.vector.memset(d_bytes[:].bitcast(I32), 0)
+        nc.vector.memset(x_bytes[:].bitcast(I32), 0)
+        nc.vector.memset(key_scales[:].bitcast(I32), 0)
+
+        l_offs = load_list(offs, "l_offs")
+        x_tab = keep.tile([P, T], U32, name="x_tab", tag="table", align_bytes=64)
+        nc.sync.dma_start(x_tab[:].bitcast(I32), words_of(x_words))
+        l_k1 = load_list(k1, "l_k1")
+        d_tab = keep.tile([P, G], U32, name="d_tab", align_bytes=64)
+        nc.sync.dma_start(d_tab[:].bitcast(I32), words_of(d_words))
+        l_two = load_list(two, "l_two")
+        nc.scalar.dma_start(d_bytes[0:P:8, :].bitcast(I32), d_scales[0].bitcast(I32))
+        for q in range(4):
+            nc.scalar.dma_start(x_bytes[32 * q : 32 * q + 4, :].bitcast(I32), x_scales[0, 4 * q : 4 * q + 4, :].bitcast(I32))
+        gn_t = keep.tile([P, PACK], F32, name="gn_t")
+        nc.gpsimd.dma_start(gn_t[:], gn.rearrange("(p t) o -> p (t o)", t=PACK))
+        gm_t = keep.tile([P, PACK], F32, name="gm_t")
+        nc.gpsimd.dma_start(gm_t[:], gm.rearrange("(p t) o -> p (t o)", t=PACK))
+        l_n1 = load_list(n1, "l_n1")
+        l_n2 = load_list(n2, "l_n2")
+        l_n3 = load_list(n3, "l_n3")
+        l_n4 = load_list(n4, "l_n4")
+        l_n5 = load_list(n5, "l_n5")
+
+        def pick_codes(offsets, name):
+            codes = keep.tile([P, S], U32, name=name, align_bytes=64)
+            nc.vector.tensor_copy(codes[:], x_tab[:].indirect(offsets[:]))
+            return codes
+
+        def pick_scales(offsets, name):
+            scales = keep.tile([P, S], U8, name=name, align_bytes=64)
+            nc.vector.tensor_copy(scales[:], x_bytes[:].indirect(offsets[:]))
+            return scales
+
+        idx_codes = pick_codes(l_offs, "idx_codes")
+        key_bytes = keep.tile([P, H], U8, name="key_bytes", align_bytes=64)
+        nc.vector.tensor_copy(key_bytes[:], d_bytes[:].indirect(l_k1[:]))
+        key_bytes_dealt = keep.tile([P, H], U8, name="key_bytes_dealt", tag="bytes", align_bytes=64)
+        deal(key_bytes_dealt[:], key_bytes[:])
+        for r in range(4):
+            queue = nc.sync if r % 2 == 0 else nc.scalar
+            queue.dma_start(key_scales[r:P:32, :].bitcast(I32), key_bytes_dealt[8 * r : P : 32, :].bitcast(I32))
+
+        idx_scales = pick_scales(l_offs, "idx_scales")
+        key_words = keep.tile([P, H], U32, name="key_words", align_bytes=64)
+        nc.vector.tensor_copy(key_words[:], d_tab[:].indirect(l_k1[:]))
+        key_codes = keep.tile([P, H], U32, name="key_codes", align_bytes=64)
+        deal(key_codes[:], key_words[:])
+
+        def score(t, codes, scales, tag):
+            bank = psum.tile([P, S], F32, name="bank", tag=tag)
+            cols = slice(P * t, P * (t + 1))
+            nc.tensor.matmul_mx(out=bank[:], lhsT=key_codes[:, cols].bitcast(FP8X4), lhsT_scale=key_scales[:, cols],
+                                rhs=codes[:].bitcast(FP8X4), rhs_scale=scales[:], start=True, stop=True)
+            return bank
+
+        a_banks = [score(t, idx_codes, idx_scales, "bank%d" % t) for t in range(PACK)]
+        two_codes = pick_codes(l_two, "two_codes")
+        two_scales = pick_scales(l_two, "two_scales")
+        b_banks = [score(t, two_codes, two_scales, "bank%d" % (PACK + t)) for t in range(PACK)]
+
+        gm_neg = keep.tile([P, PACK], F32, name="gm_neg")
+        nc.vector.tensor_scalar(gm_neg[:], gm_t[:], -0.0625, None, ALU.mult)
+        gn_neg = keep.tile([P, PACK], F32, name="gn_neg")
+        nc.vector.tensor_scalar(gn_neg[:], gn_t[:], -0.0625, None, ALU.mult)
+
+        w_tab = keep.tile([P, 2, N], U32, name="w_tab", tag="table", align_bytes=64)
+        w_bytes = keep.tile([P, N], U8, name="w_bytes", tag="bytes", align_bytes=64)
+        nc.vector.memset(w_bytes[:].bitcast(I32), 0)
+        identity = keep.tile([P, P], F32, name="identity")
+        make_identity(nc, identity[:])
+        nc.sync.dma_start(w_tab[:, 0, :].bitcast(I32), words_of(w1_words))
+        nc.sync.dma_start(w_tab[:, 1, :].bitcast(I32), words_of(w2_words))
+        for w, scales in enumerate((w1_scales, w2_scales)):
+            for q in range(4):
+                nc.sync.dma_start(w_bytes[32 * q + 4 * w : 32 * q + 4 * w + 4, :].bitcast(I32), scales[0, 4 * q : 4 * q + 4, :].bitcast(I32))
+
+        def half_of(offsets, u):
+            return offsets[:, 16 * u : 16 * (u + 1)]
+
+        halves = [slice(HALF * u, HALF * (u + 1)) for u in range(2)]
+        blocks = [slice(P * j, P * (j + 1)) for j in range(PACK)]
+        a_win = [keep.tile([P, S], F32, name="a_win%d" % t) for t in range(PACK)]
+        a_n1 = [keep.tile([P, S], F32, name="a_n1_%d" % t) for t in range(PACK)]
+        z = keep.tile([P, PACK, S], F32, name="z")
+        for t in range(PACK):
+            nc.scalar.activation(a_win[t][:], a_banks[t][:], ACT.Copy, scale=gn_neg[:, t : t + 1])
+            for u in range(2):
+                nc.scalar.activation(a_n1[t][:, halves[u]], a_win[t][:].indirect(half_of(l_n1, u)), ACT.Copy)
+                nc.vector.tensor_tensor(z[:, t, halves[u]], a_win[t][:].indirect(half_of(l_n2, u)), a_n1[t][:, halves[u]], ALU.subtract)
+
+        ex = [keep.tile([P, S], F32, name="ex%d" % t) for t in range(PACK)]
+        b_win = [keep.tile([P, S], F32, name="b_win%d" % t) for t in range(PACK)]
+        ex_n3 = [keep.tile([P, S], F32, name="ex_n3_%d" % t) for t in range(PACK)]
+        b_n4 = [keep.tile([P, S], F32, name="b_n4_%d" % t) for t in range(PACK)]
+        for t in range(PACK):
+            nc.scalar.activation(b_win[t][:], b_banks[t][:], ACT.Copy, scale=gm_neg[:, t : t + 1])
+            nc.scalar.activation(ex[t][:], b_banks[t][:], ACT.Exp, scale=0.0625)
+        for u in range(2):
+            for t in range(PACK):
+                nc.scalar.activation(ex_n3[t][:, halves[u]], ex[t][:].indirect(half_of(l_n3, u)), ACT.Copy)
+
+        z_round = keep.tile([P, PACK * S], BF16, name="z_round", align_bytes=64)
+        interleave(z_round[:], z[:])
+        for u in range(2):
+            for t in range(PACK):
+                nc.vector.tensor_copy(b_n4[t][:, halves[u]], b_win[t][:].indirect(half_of(l_n4, u)))
+        z_codes = keep.tile([P, S], U32, name="z_codes", align_bytes=64)
+        z_scales = keep.tile([P, S], U8, name="z_scales", align_bytes=64)
+        nc.vector.quantize_mx(out=z_codes[:].bitcast(FP8X4), scales=z_scales[:], in_=z_round[:])
+        w_codes = keep.tile([P, 2, N], U32, name="w_codes", align_bytes=64)
+        for w in range(2):
+            deal(w_codes[:, w, :], w_tab[:, w, :])
+        w_scales = keep.tile([P, N], U8, name="w_scales", align_bytes=64)
+        deal(w_scales[:], w_bytes[:])
+
+        logs = [keep.tile([P, S], F32, name="logs%d" % j) for j in range(PACK)]
+        for j in range(PACK):
+            total = psum.tile([P, S], F32, name="total", tag="bank%d" % j)
+            for t in range(PACK):
+                nc.tensor.matmul(total[:, blocks[t]], ex[t][:, blocks[j]], identity[:], start=True, stop=False, is_transpose=True)
+                nc.tensor.matmul(total[:, blocks[t]], ex_n3[t][:, blocks[j]], identity[:], start=False, stop=True, is_transpose=True)
+            nc.scalar.activation(logs[j][:], total[:], ACT.Ln)
+
+        h_win = [keep.tile([P, S + SPARE], F32, name="h_win%d" % t) for t in range(PACK)]
+        for t in range(PACK):
+            nc.gpsimd.memset(h_win[t][:, S:], 0.0)
+        z2_planes = []
+        for u in range(2):
+            z2 = keep.tile([P, PACK, HALF], F32, name="z2_%d" % u)
+            for pair in range(2):
+                back = psum.tile([P, 2, HALF], F32, name="back", tag="bank%d" % (PACK + 2 * u + pair))
+                for s in range(2):
+                    for i in range(2):
+                        nc.tensor.transpose(back[:, s, blocks[i]], logs[2 * u + i][:, blocks[2 * pair + s]], identity[:])
+                for s in range(2):
+                    t = 2 * pair + s
+                    nc.vector.scalar_tensor_tensor(z2[:, t, :], back[:, s, :], gm_t[:, t : t + 1], b_n4[t][:, halves[u]], ALU.mult, ALU.add)
+            z2_round = keep.tile([P, PACK * HALF], BF16, name="z2_round%d" % u, align_bytes=64)
+            interleave(z2_round[:], z2[:])
+            z2_codes = keep.tile([P, HALF], U32, name="z2_codes%d" % u, align_bytes=64)
+            z2_scales = keep.tile([P, HALF], U8, name="z2_scales%d" % u, align_bytes=64)
+            nc.vector.quantize_mx(out=z2_codes[:].bitcast(FP8X4), scales=z2_scales[:], in_=z2_round[:])
+            z2_planes.append((z2_codes, z2_scales))
+        h_banks = [psum.tile([P, S], F32, name="h_bank", tag="bank%d" % t) for t in range(PACK)]
+        for t in range(PACK):
+            nc.tensor.matmul_mx(out=h_banks[t][:], lhsT=w_codes[:, 0, blocks[t]].bitcast(FP8X4), lhsT_scale=w_scales[:, blocks[t]],
+                                rhs=z_codes[:].bitcast(FP8X4), rhs_scale=z_scales[:], start=True, stop=False)
+        for u in range(2):
+            z2_codes, z2_scales = z2_planes[u]
+            for t in range(PACK):
+                nc.tensor.matmul_mx(out=h_banks[t][:, halves[u]], lhsT=w_codes[:, 1, blocks[t]].bitcast(FP8X4), lhsT_scale=w_scales[4:P, blocks[t]],
+                                    rhs=z2_codes[:].bitcast(FP8X4), rhs_scale=z2_scales[:], start=False, stop=(u == 1))
+        nc.scalar.copy(h_win[0][:, 0:S], h_banks[0][:])
+        for t in range(1, PACK):
+            nc.vector.tensor_copy(h_win[t][:, 0:S], h_banks[t][:])
+
+        out_rows = out_0.rearrange("(p t) j -> p t j", t=PACK)
+        y_codes = keep.tile([P, S], U32, name="y_codes", align_bytes=64)
+        y_scales = keep.tile([P, S], U8, name="y_scales", align_bytes=64)
+        out_words = words_of(out_1)
+        places = CHUNK // 4
+        for c in range(G // CHUNK):
+            cols = slice(places * c, places * (c + 1))
+            y = ring.tile([P, PACK, places], F32, name="y")
+            for pair in range(2):
+                members = ring.tile([P, 2, CHUNK], F32, name="members")
+                for s in range(2):
+                    nc.scalar.activation(members[:, s, :], h_win[2 * pair + s][:].indirect(l_n5[:, 32 * c : 32 * (c + 1)]), ACT.Copy)
+                four = members[:].rearrange("p s (j e) -> p (s j) e", e=4)
+                high = ring.tile([P, 2 * places, 2], F32, name="high")
+                low = ring.tile([P, 2 * places, 2], F32, name="low")
+                nc.vector.tensor_tensor(high[:], four[:, :, 0:2], four[:, :, 2:4], ALU.max)
+                nc.vector.tensor_tensor(low[:], four[:, :, 0:2], four[:, :, 2:4], ALU.min)
+                mx = ring.tile([P, 2 * places], F32, name="mx")
+                mn = ring.tile([P, 2 * places], F32, name="mn")
+                nc.vector.tensor_tensor(mn[:], low[:, :, 0], low[:, :, 1], ALU.min)
+                nc.vector.tensor_tensor(mx[:], high[:, :, 0], high[:, :, 1], ALU.max)
+                nc.vector.scalar_tensor_tensor(y[:, 2 * pair : 2 * pair + 2, :].rearrange("p s j -> p (s j)"), mn[:], -0.5, mx[:], ALU.mult, ALU.add)
+            nc.sync.dma_start(out_rows[:, :, cols], y[:])
+            y_round = ring.tile([P, PACK * places], BF16, name="y_round", align_bytes=64)
+            interleave(y_round[:], y[:])
+            nc.vector.quantize_mx(out=y_codes[:, cols].bitcast(FP8X4), scales=y_scales[:, cols], in_=y_round[:])
+            nc.sync.dma_start(out_words[:, cols], y_codes[:, cols].bitcast(I32))
+        for q in range(4):
+            queue = nc.sync if q % 2 == 0 else nc.scalar
+            queue.dma_start(out_2[0, 4 * q : 4 * q + 4, :].bitcast(I32), y_scales[32 * q : 32 * q + 4, :].bitcast(I32))

@@ -31,8 +31,8 @@ def tile_picked_kjgaplsegspan_none_po_kernel(tc, x_words, x_scales, d_words, d_s
     def deal(dst, src):
         nc.vector.tensor_copy(out=dst.rearrange("p (t m) -> p t m", t=PACK), in_=src.rearrange("p (m t) -> p t m", t=PACK))
 
-    def interleave(dst, src):
-        nc.vector.tensor_copy(out=dst.rearrange("p (c i t) -> p c t i", i=4, t=PACK), in_=src.rearrange("p t (c i) -> p c t i", i=4))
+    def interleave(dst, src, copy=nc.vector.tensor_copy):
+        copy(out=dst.rearrange("p (c i t) -> p c t i", i=4, t=PACK), in_=src.rearrange("p t (c i) -> p c t i", i=4))
 
     with ExitStack() as ctx:
         lists = ctx.enter_context(tc.tile_pool(name="lists", bufs=1))
@@ -45,20 +45,20 @@ def tile_picked_kjgaplsegspan_none_po_kernel(tc, x_words, x_scales, d_words, d_s
             nc.sync.dma_start(tile[:], dram)
             return tile
 
-        d_bytes = keep.tile([P, G], U8, name="d_bytes", align_bytes=64)
+        d_bytes = keep.tile([P, G], U8, name="d_bytes", tag="d_bytes", align_bytes=64)
         x_bytes = keep.tile([P, T], U8, name="x_bytes", align_bytes=64)
         key_scales = keep.tile([P, H], U8, name="key_scales", align_bytes=64)
         nc.vector.memset(d_bytes[:].bitcast(I32), 0)
         nc.vector.memset(x_bytes[:].bitcast(I32), 0)
-        nc.vector.memset(key_scales[:].bitcast(I32), 0)
+        nc.gpsimd.memset(key_scales[:].bitcast(I32), 0)
 
-        l_offs = load_list(offs, "l_offs")
+        l_two = load_list(two, "l_two")
         x_tab = keep.tile([P, T], U32, name="x_tab", tag="table", align_bytes=64)
         nc.sync.dma_start(x_tab[:].bitcast(I32), words_of(x_words))
         l_k1 = load_list(k1, "l_k1")
         d_tab = keep.tile([P, G], U32, name="d_tab", align_bytes=64)
         nc.sync.dma_start(d_tab[:].bitcast(I32), words_of(d_words))
-        l_two = load_list(two, "l_two")
+        l_offs = load_list(offs, "l_offs")
         nc.scalar.dma_start(d_bytes[0:P:8, :].bitcast(I32), d_scales[0].bitcast(I32))
         for q in range(4):
             nc.scalar.dma_start(x_bytes[32 * q : 32 * q + 4, :].bitcast(I32), x_scales[0, 4 * q : 4 * q + 4, :].bitcast(I32))
@@ -66,33 +66,32 @@ def tile_picked_kjgaplsegspan_none_po_kernel(tc, x_words, x_scales, d_words, d_s
         nc.gpsimd.dma_start(gn_t[:], gn.rearrange("(p t) o -> p (t o)", t=PACK))
         gm_t = keep.tile([P, PACK], F32, name="gm_t")
         nc.gpsimd.dma_start(gm_t[:], gm.rearrange("(p t) o -> p (t o)", t=PACK))
-        l_n1 = load_list(n1, "l_n1")
-        l_n2 = load_list(n2, "l_n2")
         l_n3 = load_list(n3, "l_n3")
         l_n4 = load_list(n4, "l_n4")
+        l_n1 = load_list(n1, "l_n1")
+        l_n2 = load_list(n2, "l_n2")
         l_n5 = load_list(n5, "l_n5")
 
-        def pick_codes(offsets, name):
-            codes = keep.tile([P, S], U32, name=name, align_bytes=64)
+        def pick_codes(offsets, name, tag):
+            codes = keep.tile([P, S], U32, name=name, tag=tag, align_bytes=64)
             nc.vector.tensor_copy(codes[:], x_tab[:].indirect(offsets[:]))
             return codes
 
-        def pick_scales(offsets, name):
-            scales = keep.tile([P, S], U8, name=name, align_bytes=64)
+        def pick_scales(offsets, name, tag):
+            scales = keep.tile([P, S], U8, name=name, tag=tag, align_bytes=64)
             nc.vector.tensor_copy(scales[:], x_bytes[:].indirect(offsets[:]))
             return scales
 
-        idx_codes = pick_codes(l_offs, "idx_codes")
-        key_bytes = keep.tile([P, H], U8, name="key_bytes", align_bytes=64)
+        two_codes = pick_codes(l_two, "two_codes", "two_codes")
+        key_bytes = keep.tile([P, H], U8, name="key_bytes", tag="key_picked", align_bytes=64)
         nc.vector.tensor_copy(key_bytes[:], d_bytes[:].indirect(l_k1[:]))
         key_bytes_dealt = keep.tile([P, H], U8, name="key_bytes_dealt", tag="bytes", align_bytes=64)
         deal(key_bytes_dealt[:], key_bytes[:])
         for r in range(4):
-            queue = nc.sync if r % 2 == 0 else nc.scalar
-            queue.dma_start(key_scales[r:P:32, :].bitcast(I32), key_bytes_dealt[8 * r : P : 32, :].bitcast(I32))
+            nc.scalar.dma_start(key_scales[r:P:32, :].bitcast(I32), key_bytes_dealt[8 * r : P : 32, :].bitcast(I32))
 
-        idx_scales = pick_scales(l_offs, "idx_scales")
-        key_words = keep.tile([P, H], U32, name="key_words", align_bytes=64)
+        two_scales = pick_scales(l_two, "two_scales", "d_bytes")
+        key_words = keep.tile([P, H], U32, name="key_words", tag="key_picked", align_bytes=64)
         nc.vector.tensor_copy(key_words[:], d_tab[:].indirect(l_k1[:]))
         key_codes = keep.tile([P, H], U32, name="key_codes", align_bytes=64)
         deal(key_codes[:], key_words[:])
@@ -104,10 +103,10 @@ def tile_picked_kjgaplsegspan_none_po_kernel(tc, x_words, x_scales, d_words, d_s
                                 rhs=codes[:].bitcast(FP8X4), rhs_scale=scales[:], start=True, stop=True)
             return bank
 
-        a_banks = [score(t, idx_codes, idx_scales, "bank%d" % t) for t in range(PACK)]
-        two_codes = pick_codes(l_two, "two_codes")
-        two_scales = pick_scales(l_two, "two_scales")
-        b_banks = [score(t, two_codes, two_scales, "bank%d" % (PACK + t)) for t in range(PACK)]
+        b_banks = [score(t, two_codes, two_scales, "bank%d" % t) for t in range(PACK)]
+        idx_codes = pick_codes(l_offs, "idx_codes", "key_picked")
+        idx_scales = pick_scales(l_offs, "idx_scales", "idx_scales")
+        a_banks = [score(t, idx_codes, idx_scales, "bank%d" % (PACK + t)) for t in range(PACK)]
 
         gm_neg = keep.tile([P, PACK], F32, name="gm_neg")
         nc.vector.tensor_scalar(gm_neg[:], gm_t[:], -0.0625, None, ALU.mult)
@@ -130,34 +129,17 @@ def tile_picked_kjgaplsegspan_none_po_kernel(tc, x_words, x_scales, d_words, d_s
 
         halves = [slice(HALF * u, HALF * (u + 1)) for u in range(2)]
         blocks = [slice(P * j, P * (j + 1)) for j in range(PACK)]
-        a_win = [keep.tile([P, S], F32, name="a_win%d" % t) for t in range(PACK)]
-        a_n1 = [keep.tile([P, S], F32, name="a_n1_%d" % t) for t in range(PACK)]
-        z = keep.tile([P, PACK, S], F32, name="z")
-        for t in range(PACK):
-            nc.scalar.activation(a_win[t][:], a_banks[t][:], ACT.Copy, scale=gn_neg[:, t : t + 1])
-            for u in range(2):
-                nc.scalar.activation(a_n1[t][:, halves[u]], a_win[t][:].indirect(half_of(l_n1, u)), ACT.Copy)
-                nc.vector.tensor_tensor(z[:, t, halves[u]], a_win[t][:].indirect(half_of(l_n2, u)), a_n1[t][:, halves[u]], ALU.subtract)
-
         ex = [keep.tile([P, S], F32, name="ex%d" % t) for t in range(PACK)]
         b_win = [keep.tile([P, S], F32, name="b_win%d" % t) for t in range(PACK)]
         ex_n3 = [keep.tile([P, S], F32, name="ex_n3_%d" % t) for t in range(PACK)]
         b_n4 = [keep.tile([P, S], F32, name="b_n4_%d" % t) for t in range(PACK)]
         for t in range(PACK):
-            nc.scalar.activation(b_win[t][:], b_banks[t][:], ACT.Copy, scale=gm_neg[:, t : t + 1])
             nc.scalar.activation(ex[t][:], b_banks[t][:], ACT.Exp, scale=0.0625)
+            nc.vector.tensor_scalar(b_win[t][:], b_banks[t][:], gm_neg[:, t : t + 1], None, ALU.mult)
         for u in range(2):
             for t in range(PACK):
                 nc.scalar.activation(ex_n3[t][:, halves[u]], ex[t][:].indirect(half_of(l_n3, u)), ACT.Copy)
-
-        z_round = keep.tile([P, PACK * S], BF16, name="z_round", align_bytes=64)
-        interleave(z_round[:], z[:])
-        for u in range(2):
-            for t in range(PACK):
                 nc.vector.tensor_copy(b_n4[t][:, halves[u]], b_win[t][:].indirect(half_of(l_n4, u)))
-        z_codes = keep.tile([P, S], U32, name="z_codes", align_bytes=64)
-        z_scales = keep.tile([P, S], U8, name="z_scales", align_bytes=64)
-        nc.vector.quantize_mx(out=z_codes[:].bitcast(FP8X4), scales=z_scales[:], in_=z_round[:])
         w_codes = keep.tile([P, 2, N], U32, name="w_codes", align_bytes=64)
         for w in range(2):
             deal(w_codes[:, w, :], w_tab[:, w, :])
@@ -172,47 +154,97 @@ def tile_picked_kjgaplsegspan_none_po_kernel(tc, x_words, x_scales, d_words, d_s
                 nc.tensor.matmul(total[:, blocks[t]], ex_n3[t][:, blocks[j]], identity[:], start=False, stop=True, is_transpose=True)
             nc.scalar.activation(logs[j][:], total[:], ACT.Ln)
 
-        h_win = [keep.tile([P, S + SPARE], F32, name="h_win%d" % t) for t in range(PACK)]
-        for t in range(PACK):
-            nc.gpsimd.memset(h_win[t][:, S:], 0.0)
-        z2_planes = []
+        def planes(name):
+            rounded = keep.tile([P, PACK * HALF], BF16, name=name + "_round", align_bytes=64)
+            codes = keep.tile([P, HALF], U32, name=name + "_codes", align_bytes=64)
+            scales = keep.tile([P, HALF], U8, name=name + "_scales", align_bytes=64)
+            return rounded, codes, scales
+
+        def quantise(rounded, codes, scales):
+            nc.vector.quantize_mx(out=codes.bitcast(FP8X4), scales=scales, in_=rounded)
+
+        z2 = [keep.tile([P, PACK, HALF], F32, name="z2_%d" % u) for u in range(2)]
+        z2_planes = [planes("z2_%d" % u) for u in range(2)]
         for u in range(2):
-            z2 = keep.tile([P, PACK, HALF], F32, name="z2_%d" % u)
             for pair in range(2):
-                back = psum.tile([P, 2, HALF], F32, name="back", tag="bank%d" % (PACK + 2 * u + pair))
+                back = psum.tile([P, 2, HALF], F32, name="back", tag="bank%d" % (2 * u + pair))
                 for s in range(2):
                     for i in range(2):
                         nc.tensor.transpose(back[:, s, blocks[i]], logs[2 * u + i][:, blocks[2 * pair + s]], identity[:])
                 for s in range(2):
                     t = 2 * pair + s
-                    nc.vector.scalar_tensor_tensor(z2[:, t, :], back[:, s, :], gm_t[:, t : t + 1], b_n4[t][:, halves[u]], ALU.mult, ALU.add)
-            z2_round = keep.tile([P, PACK * HALF], BF16, name="z2_round%d" % u, align_bytes=64)
-            interleave(z2_round[:], z2[:])
-            z2_codes = keep.tile([P, HALF], U32, name="z2_codes%d" % u, align_bytes=64)
-            z2_scales = keep.tile([P, HALF], U8, name="z2_scales%d" % u, align_bytes=64)
-            nc.vector.quantize_mx(out=z2_codes[:].bitcast(FP8X4), scales=z2_scales[:], in_=z2_round[:])
-            z2_planes.append((z2_codes, z2_scales))
-        h_banks = [psum.tile([P, S], F32, name="h_bank", tag="bank%d" % t) for t in range(PACK)]
-        for t in range(PACK):
-            nc.tensor.matmul_mx(out=h_banks[t][:], lhsT=w_codes[:, 0, blocks[t]].bitcast(FP8X4), lhsT_scale=w_scales[:, blocks[t]],
-                                rhs=z_codes[:].bitcast(FP8X4), rhs_scale=z_scales[:], start=True, stop=False)
+                    nc.vector.scalar_tensor_tensor(z2[u][:, t, :], back[:, s, :], gm_t[:, t : t + 1], b_n4[t][:, halves[u]], ALU.mult, ALU.add)
         for u in range(2):
-            z2_codes, z2_scales = z2_planes[u]
-            for t in range(PACK):
-                nc.tensor.matmul_mx(out=h_banks[t][:, halves[u]], lhsT=w_codes[:, 1, blocks[t]].bitcast(FP8X4), lhsT_scale=w_scales[4:P, blocks[t]],
-                                    rhs=z2_codes[:].bitcast(FP8X4), rhs_scale=z2_scales[:], start=False, stop=(u == 1))
-        nc.scalar.copy(h_win[0][:, 0:S], h_banks[0][:])
+            interleave(z2_planes[u][0][:], z2[u][:])
+        for u in range(2):
+            quantise(*[tile[:] for tile in z2_planes[u]])
+
+        a_win = [keep.tile([P, S], F32, name="a_win%d" % t) for t in range(PACK)]
+        a_n1 = [keep.tile([P, S], F32, name="a_n1_%d" % t) for t in range(PACK)]
+        z = [keep.tile([P, PACK, HALF], F32, name="z%d" % u) for u in range(2)]
+        z_planes = [planes("z_%d" % u) for u in range(2)]
+        h_win = [keep.tile([P, S + SPARE], F32, name="h_win%d" % t) for t in range(PACK)]
+        for t in range(PACK):
+            nc.gpsimd.memset(h_win[t][:, S:], 0.0)
+
+        def look_up_a(t, u):
+            nc.scalar.activation(a_n1[t][:, halves[u]], a_win[t][:].indirect(half_of(l_n1, u)), ACT.Copy)
+            nc.vector.tensor_tensor(z[u][:, t, :], a_win[t][:].indirect(half_of(l_n2, u)), a_n1[t][:, halves[u]], ALU.subtract)
+
+        def add_pass(out, w, t, operand, start, stop):
+            nc.tensor.matmul_mx(out=out, lhsT=w_codes[:, w, blocks[t]].bitcast(FP8X4), lhsT_scale=w_scales[4 * w : P, blocks[t]],
+                                rhs=operand[1][:].bitcast(FP8X4), rhs_scale=operand[2][:], start=start, stop=stop)
+
+        def leave_a(t):
+            nc.scalar.activation(a_win[t][:], a_banks[t][:], ACT.Copy, scale=gn_neg[:, t : t + 1])
+
+        leave_a(0)
+        for t in range(PACK):
+            if t + 1 < PACK:
+                leave_a(t + 1)
+            look_up_a(t, 0)
+        look_up_a(0, 1)
+        interleave(z_planes[0][0][:], z[0][:])
+        look_up_a(1, 1)
+        quantise(*[tile[:] for tile in z_planes[0]])
+        look_up_a(2, 1)
+        look_up_a(3, 1)
+        h_banks = [[psum.tile([P, HALF], F32, name="h_bank", tag="bank%d" % (PACK * u + t)) for t in range(PACK)] for u in range(2)]
+        for t in range(PACK):
+            add_pass(h_banks[0][t][:], 1, t, z2_planes[0], True, False)
+            add_pass(h_banks[0][t][:], 0, t, z_planes[0], False, True)
+            nc.scalar.copy(h_win[t][:, halves[0]], h_banks[0][t][:])
+        for t in range(PACK):
+            add_pass(h_banks[1][t][:], 1, t, z2_planes[1], True, False)
+        interleave(z_planes[1][0][:], z[1][:])
+        quantise(*[tile[:] for tile in z_planes[1]])
+        for t in range(PACK):
+            add_pass(h_banks[1][t][:], 0, t, z_planes[1], False, True)
+        nc.scalar.copy(h_win[0][:, halves[1]], h_banks[1][0][:])
         for t in range(1, PACK):
-            nc.vector.tensor_copy(h_win[t][:, 0:S], h_banks[t][:])
+            nc.vector.tensor_copy(h_win[t][:, halves[1]], h_banks[1][t][:])
 
         out_rows = out_0.rearrange("(p t) j -> p t j", t=PACK)
         y_codes = keep.tile([P, S], U32, name="y_codes", align_bytes=64)
         y_scales = keep.tile([P, S], U8, name="y_scales", align_bytes=64)
         out_words = words_of(out_1)
         places = CHUNK // 4
-        for c in range(G // CHUNK):
+        chunks = G // CHUNK
+        y = [keep.tile([P, PACK, places], F32, name="y%d" % c) for c in range(chunks)]
+        y_round = [keep.tile([P, PACK * places], BF16, name="y_round%d" % c, align_bytes=64) for c in range(chunks)]
+
+        def combine(c, pair, mx, mn):
+            nc.vector.scalar_tensor_tensor(y[c][:, 2 * pair : 2 * pair + 2, :].rearrange("p s j -> p (s j)"), mn[:], -0.5, mx[:], ALU.mult, ALU.add)
+            if pair == 1:
+                nc.sync.dma_start(out_rows[:, :, places * c : places * (c + 1)], y[c][:])
+
+        def store_codes(c):
             cols = slice(places * c, places * (c + 1))
-            y = ring.tile([P, PACK, places], F32, name="y")
+            quantise(y_round[c][:], y_codes[:, cols], y_scales[:, cols])
+            nc.sync.dma_start(out_words[:, cols], y_codes[:, cols].bitcast(I32))
+
+        waiting = None
+        for c in range(chunks):
             for pair in range(2):
                 members = ring.tile([P, 2, CHUNK], F32, name="members")
                 for s in range(2):
@@ -220,18 +252,24 @@ def tile_picked_kjgaplsegspan_none_po_kernel(tc, x_words, x_scales, d_words, d_s
                 four = members[:].rearrange("p s (j e) -> p (s j) e", e=4)
                 high = ring.tile([P, 2 * places, 2], F32, name="high")
                 low = ring.tile([P, 2 * places, 2], F32, name="low")
-                nc.vector.tensor_tensor(high[:], four[:, :, 0:2], four[:, :, 2:4], ALU.max)
-                nc.vector.tensor_tensor(low[:], four[:, :, 0:2], four[:, :, 2:4], ALU.min)
                 mx = ring.tile([P, 2 * places], F32, name="mx")
                 mn = ring.tile([P, 2 * places], F32, name="mn")
-                nc.vector.tensor_tensor(mn[:], low[:, :, 0], low[:, :, 1], ALU.min)
+                nc.vector.tensor_tensor(high[:], four[:, :, 0:2], four[:, :, 2:4], ALU.max)
+                if waiting is not None:
+                    combine(*waiting)
+                nc.vector.tensor_tensor(low[:], four[:, :, 0:2], four[:, :, 2:4], ALU.min)
                 nc.vector.tensor_tensor(mx[:], high[:, :, 0], high[:, :, 1], ALU.max)
-                nc.vector.scalar_tensor_tensor(y[:, 2 * pair : 2 * pair + 2, :].rearrange("p s j -> p (s j)"), mn[:], -0.5, mx[:], ALU.mult, ALU.add)
-            nc.sync.dma_start(out_rows[:, :, cols], y[:])
-            y_round = ring.tile([P, PACK * places], BF16, name="y_round", align_bytes=64)
-            interleave(y_round[:], y[:])
-            nc.vector.quantize_mx(out=y_codes[:, cols].bitcast(FP8X4), scales=y_scales[:, cols], in_=y_round[:])
-            nc.sync.dma_start(out_words[:, cols], y_codes[:, cols].bitcast(I32))
+                if 0 < c < chunks - 1 and pair == 0:
+                    interleave(y_round[c - 1][:], y[c - 1][:])
+                if 0 < c < chunks - 1 and pair == 1:
+                    store_codes(c - 1)
+                nc.vector.tensor_tensor(mn[:], low[:, :, 0], low[:, :, 1], ALU.min)
+                waiting = (c, pair, mx, mn)
+        interleave(y_round[chunks - 2][:], y[chunks - 2][:], nc.scalar.copy)
+        store_codes(chunks - 2)
+        combine(*waiting)
+        interleave(y_round[chunks - 1][:], y[chunks - 1][:])
+        store_codes(chunks - 1)
         for q in range(4):
             queue = nc.sync if q % 2 == 0 else nc.scalar
             queue.dma_start(out_2[0, 4 * q : 4 * q + 4, :].bitcast(I32), y_scales[32 * q : 32 * q + 4, :].bitcast(I32))

@@ -29,7 +29,7 @@ def tile_picked_kjgaplsegspan_none_po_kernel(tc, x_words, x_scales, d_words, d_s
         return dram[0].rearrange("p c r -> p (c r)").bitcast(I32)
 
     def deal(dst, src):
-        nc.vector.tensor_copy(out=dst.rearrange("p (t m) -> p t m", t=PACK), in_=src.rearrange("p (m t) -> p t m", t=PACK))
+        nc.vector.tensor_copy(out=dst.rearrange("p (t c i) -> p c t i", t=PACK, i=4), in_=src.rearrange("p (c i t) -> p c t i", t=PACK, i=4))
 
     def interleave(dst, src, copy=nc.vector.tensor_copy):
         copy(out=dst.rearrange("p (c i t) -> p c t i", i=4, t=PACK), in_=src.rearrange("p t (c i) -> p c t i", i=4))
@@ -45,77 +45,75 @@ def tile_picked_kjgaplsegspan_none_po_kernel(tc, x_words, x_scales, d_words, d_s
             nc.sync.dma_start(tile[:], dram)
             return tile
 
-        d_bytes = keep.tile([P, G], U8, name="d_bytes", tag="d_bytes", align_bytes=64)
-        x_bytes = keep.tile([P, T], U8, name="x_bytes", align_bytes=64)
-        key_scales = keep.tile([P, H], U8, name="key_scales", align_bytes=64)
+        d_bytes = keep.tile([P, G], U8, name="d_bytes", align_bytes=64)
+        x_bytes = keep.tile([P, T], U8, name="x_bytes", tag="x_bytes", align_bytes=64)
         nc.vector.memset(d_bytes[:].bitcast(I32), 0)
         nc.vector.memset(x_bytes[:].bitcast(I32), 0)
-        nc.gpsimd.memset(key_scales[:].bitcast(I32), 0)
 
+        l_k1 = load_list(k1, "l_k1")
+        nc.scalar.dma_start(d_bytes[0:P:8, :].bitcast(I32), d_scales[0].bitcast(I32))
         l_two = load_list(two, "l_two")
+        nc.scalar.dma_start(x_bytes[0:P:8, :].bitcast(I32), x_scales[0].bitcast(I32))
         x_tab = keep.tile([P, T], U32, name="x_tab", tag="table", align_bytes=64)
         nc.sync.dma_start(x_tab[:].bitcast(I32), words_of(x_words))
-        l_k1 = load_list(k1, "l_k1")
-        d_tab = keep.tile([P, G], U32, name="d_tab", align_bytes=64)
-        nc.sync.dma_start(d_tab[:].bitcast(I32), words_of(d_words))
         l_offs = load_list(offs, "l_offs")
-        nc.scalar.dma_start(d_bytes[0:P:8, :].bitcast(I32), d_scales[0].bitcast(I32))
-        for q in range(4):
-            nc.scalar.dma_start(x_bytes[32 * q : 32 * q + 4, :].bitcast(I32), x_scales[0, 4 * q : 4 * q + 4, :].bitcast(I32))
-        gn_t = keep.tile([P, PACK], F32, name="gn_t")
-        nc.gpsimd.dma_start(gn_t[:], gn.rearrange("(p t) o -> p (t o)", t=PACK))
         gm_t = keep.tile([P, PACK], F32, name="gm_t")
         nc.gpsimd.dma_start(gm_t[:], gm.rearrange("(p t) o -> p (t o)", t=PACK))
+        gn_t = keep.tile([P, PACK], F32, name="gn_t")
+        nc.gpsimd.dma_start(gn_t[:], gn.rearrange("(p t) o -> p (t o)", t=PACK))
         l_n3 = load_list(n3, "l_n3")
         l_n4 = load_list(n4, "l_n4")
         l_n1 = load_list(n1, "l_n1")
+        d_tab = keep.tile([P, G], U32, name="d_tab", align_bytes=64)
+        nc.sync.dma_start(d_tab[:].bitcast(I32), words_of(d_words))
         l_n2 = load_list(n2, "l_n2")
         l_n5 = load_list(n5, "l_n5")
 
-        def pick_codes(offsets, name, tag):
-            codes = keep.tile([P, S], U32, name=name, tag=tag, align_bytes=64)
-            nc.vector.tensor_copy(codes[:], x_tab[:].indirect(offsets[:]))
-            return codes
+        def pick(table, offsets, dtype, name, tag):
+            picked = keep.tile([P, S], dtype, name=name, tag=tag, align_bytes=64)
+            nc.vector.tensor_copy(picked[:], table[:].indirect(offsets[:]))
+            return picked
 
-        def pick_scales(offsets, name, tag):
-            scales = keep.tile([P, S], U8, name=name, tag=tag, align_bytes=64)
-            nc.vector.tensor_copy(scales[:], x_bytes[:].indirect(offsets[:]))
-            return scales
+        def place_rows(plane, queues):
+            for r in range(1, 4):
+                queues[r - 1].dma_start(plane[r:P:32, :].bitcast(I32), plane[8 * r : P : 32, :].bitcast(I32))
 
-        two_codes = pick_codes(l_two, "two_codes", "two_codes")
-        key_bytes = keep.tile([P, H], U8, name="key_bytes", tag="key_picked", align_bytes=64)
-        nc.vector.tensor_copy(key_bytes[:], d_bytes[:].indirect(l_k1[:]))
-        key_bytes_dealt = keep.tile([P, H], U8, name="key_bytes_dealt", tag="bytes", align_bytes=64)
-        deal(key_bytes_dealt[:], key_bytes[:])
-        for r in range(4):
-            nc.scalar.dma_start(key_scales[r:P:32, :].bitcast(I32), key_bytes_dealt[8 * r : P : 32, :].bitcast(I32))
-
-        two_scales = pick_scales(l_two, "two_scales", "d_bytes")
-        key_words = keep.tile([P, H], U32, name="key_words", tag="key_picked", align_bytes=64)
-        nc.vector.tensor_copy(key_words[:], d_tab[:].indirect(l_k1[:]))
+        first_scales = keep.tile([P, H + S], U8, name="first_scales", align_bytes=64)
+        key_scales = first_scales[:, 0:H]
+        two_scales = first_scales[:, H:]
+        key_bytes = pick(d_bytes, l_k1, U8, "key_bytes", "picked_first")
+        two_bytes = pick(x_bytes, l_two, U8, "two_bytes", "picked_second")
+        deal(key_scales, key_bytes[:])
+        nc.vector.tensor_copy(two_scales.bitcast(I32), two_bytes[:].bitcast(I32))
+        place_rows(first_scales, (nc.scalar, nc.sync, nc.sync))
+        two_codes = pick(x_tab, l_two, U32, "two_codes", "picked_first")
+        key_words = pick(d_tab, l_k1, U32, "key_words", "picked_second")
         key_codes = keep.tile([P, H], U32, name="key_codes", align_bytes=64)
         deal(key_codes[:], key_words[:])
+        idx_bytes = pick(x_bytes, l_offs, U8, "idx_bytes", "picked_second")
 
         def score(t, codes, scales, tag):
             bank = psum.tile([P, S], F32, name="bank", tag=tag)
             cols = slice(P * t, P * (t + 1))
             nc.tensor.matmul_mx(out=bank[:], lhsT=key_codes[:, cols].bitcast(FP8X4), lhsT_scale=key_scales[:, cols],
-                                rhs=codes[:].bitcast(FP8X4), rhs_scale=scales[:], start=True, stop=True)
+                                rhs=codes[:].bitcast(FP8X4), rhs_scale=scales, start=True, stop=True)
             return bank
 
         b_banks = [score(t, two_codes, two_scales, "bank%d" % t) for t in range(PACK)]
-        idx_codes = pick_codes(l_offs, "idx_codes", "key_picked")
-        idx_scales = pick_scales(l_offs, "idx_scales", "idx_scales")
-        a_banks = [score(t, idx_codes, idx_scales, "bank%d" % (PACK + t)) for t in range(PACK)]
+        idx_scales = keep.tile([P, S], U8, name="idx_scales", align_bytes=64)
+        nc.vector.tensor_copy(idx_scales[:].bitcast(I32), idx_bytes[:].bitcast(I32))
+        place_rows(idx_scales, (nc.sync, nc.sync, nc.sync))
+        idx_codes = pick(x_tab, l_offs, U32, "idx_codes", "picked_second")
+        a_banks = [score(t, idx_codes, idx_scales[:], "bank%d" % (PACK + t)) for t in range(PACK)]
 
         gm_neg = keep.tile([P, PACK], F32, name="gm_neg")
-        nc.vector.tensor_scalar(gm_neg[:], gm_t[:], -0.0625, None, ALU.mult)
+        nc.gpsimd.tensor_scalar(gm_neg[:], gm_t[:], -0.0625, None, ALU.mult)
         gn_neg = keep.tile([P, PACK], F32, name="gn_neg")
-        nc.vector.tensor_scalar(gn_neg[:], gn_t[:], -0.0625, None, ALU.mult)
+        nc.gpsimd.tensor_scalar(gn_neg[:], gn_t[:], -0.0625, None, ALU.mult)
 
         w_tab = keep.tile([P, 2, N], U32, name="w_tab", tag="table", align_bytes=64)
-        w_bytes = keep.tile([P, N], U8, name="w_bytes", tag="bytes", align_bytes=64)
-        nc.vector.memset(w_bytes[:].bitcast(I32), 0)
+        w_bytes = keep.tile([P, N], U8, name="w_bytes", tag="x_bytes", align_bytes=64)
+        nc.gpsimd.memset(w_bytes[:].bitcast(I32), 0)
         identity = keep.tile([P, P], F32, name="identity")
         make_identity(nc, identity[:])
         nc.sync.dma_start(w_tab[:, 0, :].bitcast(I32), words_of(w1_words))
@@ -147,12 +145,14 @@ def tile_picked_kjgaplsegspan_none_po_kernel(tc, x_words, x_scales, d_words, d_s
         deal(w_scales[:], w_bytes[:])
 
         logs = [keep.tile([P, S], F32, name="logs%d" % j) for j in range(PACK)]
-        for j in range(PACK):
-            total = psum.tile([P, S], F32, name="total", tag="bank%d" % j)
+        totals = [psum.tile([P, S], F32, name="total", tag="bank%d" % j) for j in range(PACK)]
+        for u in range(2):
             for t in range(PACK):
-                nc.tensor.matmul(total[:, blocks[t]], ex[t][:, blocks[j]], identity[:], start=True, stop=False, is_transpose=True)
-                nc.tensor.matmul(total[:, blocks[t]], ex_n3[t][:, blocks[j]], identity[:], start=False, stop=True, is_transpose=True)
-            nc.scalar.activation(logs[j][:], total[:], ACT.Ln)
+                for j in (2 * u, 2 * u + 1):
+                    nc.tensor.matmul(totals[j][:, blocks[t]], ex[t][:, blocks[j]], identity[:], start=True, stop=False, is_transpose=True)
+                    nc.tensor.matmul(totals[j][:, blocks[t]], ex_n3[t][:, blocks[j]], identity[:], start=False, stop=True, is_transpose=True)
+        for j in range(PACK):
+            nc.scalar.activation(logs[j][:], totals[j][:], ACT.Ln)
 
         def planes(name):
             rounded = keep.tile([P, PACK * HALF], BF16, name=name + "_round", align_bytes=64)
@@ -174,10 +174,7 @@ def tile_picked_kjgaplsegspan_none_po_kernel(tc, x_words, x_scales, d_words, d_s
                 for s in range(2):
                     t = 2 * pair + s
                     nc.vector.scalar_tensor_tensor(z2[u][:, t, :], back[:, s, :], gm_t[:, t : t + 1], b_n4[t][:, halves[u]], ALU.mult, ALU.add)
-        for u in range(2):
-            interleave(z2_planes[u][0][:], z2[u][:])
-        for u in range(2):
-            quantise(*[tile[:] for tile in z2_planes[u]])
+        interleave(z2_planes[0][0][:], z2[0][:])
 
         a_win = [keep.tile([P, S], F32, name="a_win%d" % t) for t in range(PACK)]
         a_n1 = [keep.tile([P, S], F32, name="a_n1_%d" % t) for t in range(PACK)]
@@ -203,12 +200,14 @@ def tile_picked_kjgaplsegspan_none_po_kernel(tc, x_words, x_scales, d_words, d_s
             if t + 1 < PACK:
                 leave_a(t + 1)
             look_up_a(t, 0)
-        look_up_a(0, 1)
-        interleave(z_planes[0][0][:], z[0][:])
-        look_up_a(1, 1)
+            if t == 0:
+                quantise(*[tile[:] for tile in z2_planes[0]])
+        interleave(z2_planes[1][0][:], z2[1][:], nc.scalar.copy)
+        quantise(*[tile[:] for tile in z2_planes[1]])
+        for t in range(PACK):
+            look_up_a(t, 1)
+        interleave(z_planes[0][0][:], z[0][:], nc.scalar.copy)
         quantise(*[tile[:] for tile in z_planes[0]])
-        look_up_a(2, 1)
-        look_up_a(3, 1)
         h_banks = [[psum.tile([P, HALF], F32, name="h_bank", tag="bank%d" % (PACK * u + t)) for t in range(PACK)] for u in range(2)]
         for t in range(PACK):
             add_pass(h_banks[0][t][:], 1, t, z2_planes[0], True, False)
@@ -228,48 +227,49 @@ def tile_picked_kjgaplsegspan_none_po_kernel(tc, x_words, x_scales, d_words, d_s
         y_codes = keep.tile([P, S], U32, name="y_codes", align_bytes=64)
         y_scales = keep.tile([P, S], U8, name="y_scales", align_bytes=64)
         out_words = words_of(out_1)
-        places = CHUNK // 4
-        chunks = G // CHUNK
-        y = [keep.tile([P, PACK, places], F32, name="y%d" % c) for c in range(chunks)]
-        y_round = [keep.tile([P, PACK * places], BF16, name="y_round%d" % c, align_bytes=64) for c in range(chunks)]
+        chunks = [(0, 128, ((0, 1), (2, 3))), (128, 128, ((0, 1), (2, 3))), (256, 128, ((0, 1), (2, 3))),
+                  (384, 64, ((0, 1), (2, 3))), (448, 64, ((0, 1), (2,), (3,)))]
+        y = [keep.tile([P, PACK, places], F32, name="y%d" % c) for c, (first, places, groups) in enumerate(chunks)]
+        y_round = [keep.tile([P, PACK * places], BF16, name="y_round%d" % c, align_bytes=64) for c, (first, places, groups) in enumerate(chunks)]
 
-        def combine(c, pair, mx, mn):
-            nc.vector.scalar_tensor_tensor(y[c][:, 2 * pair : 2 * pair + 2, :].rearrange("p s j -> p (s j)"), mn[:], -0.5, mx[:], ALU.mult, ALU.add)
-            if pair == 1:
-                nc.sync.dma_start(out_rows[:, :, places * c : places * (c + 1)], y[c][:])
+        def combine(c, group, mx, mn):
+            first, places, groups = chunks[c]
+            nc.vector.scalar_tensor_tensor(y[c][:, group[0] : group[-1] + 1, :].rearrange("p s j -> p (s j)"), mn[:], -0.5, mx[:], ALU.mult, ALU.add)
+            if group == groups[-1]:
+                nc.sync.dma_start(out_rows[:, :, first : first + places], y[c][:])
 
         def store_codes(c):
-            cols = slice(places * c, places * (c + 1))
+            first, places, groups = chunks[c]
+            cols = slice(first, first + places)
             quantise(y_round[c][:], y_codes[:, cols], y_scales[:, cols])
             nc.sync.dma_start(out_words[:, cols], y_codes[:, cols].bitcast(I32))
 
         waiting = None
-        for c in range(chunks):
-            for pair in range(2):
-                members = ring.tile([P, 2, CHUNK], F32, name="members")
-                for s in range(2):
-                    nc.scalar.activation(members[:, s, :], h_win[2 * pair + s][:].indirect(l_n5[:, 32 * c : 32 * (c + 1)]), ACT.Copy)
+        for c, (first, places, groups) in enumerate(chunks):
+            for number, group in enumerate(groups):
+                width = len(group) * places
+                members = ring.tile([P, len(group), 4 * places], F32, name="members")
+                for s, t in enumerate(group):
+                    nc.scalar.activation(members[:, s, :], h_win[t][:].indirect(l_n5[:, first // 4 : (first + places) // 4]), ACT.Copy)
                 four = members[:].rearrange("p s (j e) -> p (s j) e", e=4)
-                high = ring.tile([P, 2 * places, 2], F32, name="high")
-                low = ring.tile([P, 2 * places, 2], F32, name="low")
-                mx = ring.tile([P, 2 * places], F32, name="mx")
-                mn = ring.tile([P, 2 * places], F32, name="mn")
+                high = ring.tile([P, width, 2], F32, name="high")
+                low = ring.tile([P, width, 2], F32, name="low")
+                mx = ring.tile([P, width], F32, name="mx")
+                mn = ring.tile([P, width], F32, name="mn")
                 nc.vector.tensor_tensor(high[:], four[:, :, 0:2], four[:, :, 2:4], ALU.max)
                 if waiting is not None:
                     combine(*waiting)
                 nc.vector.tensor_tensor(low[:], four[:, :, 0:2], four[:, :, 2:4], ALU.min)
                 nc.vector.tensor_tensor(mx[:], high[:, :, 0], high[:, :, 1], ALU.max)
-                if 0 < c < chunks - 1 and pair == 0:
+                if c > 0 and number == 0:
                     interleave(y_round[c - 1][:], y[c - 1][:])
-                if 0 < c < chunks - 1 and pair == 1:
+                if c > 0 and number == 1:
                     store_codes(c - 1)
                 nc.vector.tensor_tensor(mn[:], low[:, :, 0], low[:, :, 1], ALU.min)
-                waiting = (c, pair, mx, mn)
-        interleave(y_round[chunks - 2][:], y[chunks - 2][:], nc.scalar.copy)
-        store_codes(chunks - 2)
+                waiting = (c, group, mx, mn)
         combine(*waiting)
-        interleave(y_round[chunks - 1][:], y[chunks - 1][:])
-        store_codes(chunks - 1)
+        interleave(y_round[len(chunks) - 1][:], y[len(chunks) - 1][:])
+        store_codes(len(chunks) - 1)
         for q in range(4):
             queue = nc.sync if q % 2 == 0 else nc.scalar
             queue.dma_start(out_2[0, 4 * q : 4 * q + 4, :].bitcast(I32), y_scales[32 * q : 32 * q + 4, :].bitcast(I32))

@@ -45,7 +45,7 @@ def tile_picked_kjgaplsegspan_none_po_kernel(tc, x_words, x_scales, d_words, d_s
             nc.sync.dma_start(tile[:], dram)
             return tile
 
-        d_bytes = keep.tile([P, G], U8, name="d_bytes", align_bytes=64)
+        d_bytes = keep.tile([P, G], U8, name="d_bytes", tag="d_bytes", align_bytes=64)
         x_bytes = keep.tile([P, T], U8, name="x_bytes", tag="x_bytes", align_bytes=64)
         nc.vector.memset(d_bytes[:].bitcast(I32), 0)
         nc.vector.memset(x_bytes[:].bitcast(I32), 0)
@@ -53,7 +53,8 @@ def tile_picked_kjgaplsegspan_none_po_kernel(tc, x_words, x_scales, d_words, d_s
         l_k1 = load_list(k1, "l_k1")
         nc.scalar.dma_start(d_bytes[0:P:8, :].bitcast(I32), d_scales[0].bitcast(I32))
         l_two = load_list(two, "l_two")
-        nc.scalar.dma_start(x_bytes[0:P:8, :].bitcast(I32), x_scales[0].bitcast(I32))
+        for q in range(4):
+            nc.scalar.dma_start(x_bytes[32 * q : 32 * q + 4, :].bitcast(I32), x_scales[0, 4 * q : 4 * q + 4, :].bitcast(I32))
         x_tab = keep.tile([P, T], U32, name="x_tab", tag="table", align_bytes=64)
         nc.sync.dma_start(x_tab[:].bitcast(I32), words_of(x_words))
         l_offs = load_list(offs, "l_offs")
@@ -64,7 +65,7 @@ def tile_picked_kjgaplsegspan_none_po_kernel(tc, x_words, x_scales, d_words, d_s
         l_n3 = load_list(n3, "l_n3")
         l_n4 = load_list(n4, "l_n4")
         l_n1 = load_list(n1, "l_n1")
-        d_tab = keep.tile([P, G], U32, name="d_tab", align_bytes=64)
+        d_tab = keep.tile([P, G], U32, name="d_tab", tag="dictionary", align_bytes=64)
         nc.sync.dma_start(d_tab[:].bitcast(I32), words_of(d_words))
         l_n2 = load_list(n2, "l_n2")
         l_n5 = load_list(n5, "l_n5")
@@ -74,23 +75,16 @@ def tile_picked_kjgaplsegspan_none_po_kernel(tc, x_words, x_scales, d_words, d_s
             nc.vector.tensor_copy(picked[:], table[:].indirect(offsets[:]))
             return picked
 
-        def place_rows(plane, queues):
-            for r in range(1, 4):
-                queues[r - 1].dma_start(plane[r:P:32, :].bitcast(I32), plane[8 * r : P : 32, :].bitcast(I32))
-
-        first_scales = keep.tile([P, H + S], U8, name="first_scales", align_bytes=64)
-        key_scales = first_scales[:, 0:H]
-        two_scales = first_scales[:, H:]
+        key_scales = keep.tile([P, H], U8, name="key_scales", align_bytes=64)
         key_bytes = pick(d_bytes, l_k1, U8, "key_bytes", "picked_first")
-        two_bytes = pick(x_bytes, l_two, U8, "two_bytes", "picked_second")
-        deal(key_scales, key_bytes[:])
-        nc.vector.tensor_copy(two_scales.bitcast(I32), two_bytes[:].bitcast(I32))
-        place_rows(first_scales, (nc.scalar, nc.sync, nc.sync))
-        two_codes = pick(x_tab, l_two, U32, "two_codes", "picked_first")
-        key_words = pick(d_tab, l_k1, U32, "key_words", "picked_second")
+        deal(key_scales[:], key_bytes[:])
+        for r, queue in ((1, nc.scalar), (2, nc.sync), (3, nc.sync)):
+            queue.dma_start(key_scales[r:P:32, :].bitcast(I32), key_scales[8 * r : P : 32, :].bitcast(I32))
+        two_scales = pick(x_bytes, l_two, U8, "two_scales", "d_bytes")
+        two_codes = pick(x_tab, l_two, U32, "two_codes", "two_codes")
+        key_words = pick(d_tab, l_k1, U32, "key_words", "picked_first")
         key_codes = keep.tile([P, H], U32, name="key_codes", align_bytes=64)
         deal(key_codes[:], key_words[:])
-        idx_bytes = pick(x_bytes, l_offs, U8, "idx_bytes", "picked_second")
 
         def score(t, codes, scales, tag):
             bank = psum.tile([P, S], F32, name="bank", tag=tag)
@@ -99,11 +93,9 @@ def tile_picked_kjgaplsegspan_none_po_kernel(tc, x_words, x_scales, d_words, d_s
                                 rhs=codes[:].bitcast(FP8X4), rhs_scale=scales, start=True, stop=True)
             return bank
 
-        b_banks = [score(t, two_codes, two_scales, "bank%d" % t) for t in range(PACK)]
-        idx_scales = keep.tile([P, S], U8, name="idx_scales", align_bytes=64)
-        nc.vector.tensor_copy(idx_scales[:].bitcast(I32), idx_bytes[:].bitcast(I32))
-        place_rows(idx_scales, (nc.sync, nc.sync, nc.sync))
-        idx_codes = pick(x_tab, l_offs, U32, "idx_codes", "picked_second")
+        b_banks = [score(t, two_codes, two_scales[:], "bank%d" % t) for t in range(PACK)]
+        idx_scales = pick(x_bytes, l_offs, U8, "idx_scales", "picked_first")
+        idx_codes = pick(x_tab, l_offs, U32, "idx_codes", "dictionary")
         a_banks = [score(t, idx_codes, idx_scales[:], "bank%d" % (PACK + t)) for t in range(PACK)]
 
         gm_neg = keep.tile([P, PACK], F32, name="gm_neg")
@@ -144,6 +136,9 @@ def tile_picked_kjgaplsegspan_none_po_kernel(tc, x_words, x_scales, d_words, d_s
         w_scales = keep.tile([P, N], U8, name="w_scales", align_bytes=64)
         deal(w_scales[:], w_bytes[:])
 
+        a_win = [keep.tile([P, S], F32, name="a_win%d" % t) for t in range(PACK)]
+        for t in range(2):
+            nc.vector.tensor_scalar(a_win[t][:], a_banks[t][:], gn_neg[:, t : t + 1], None, ALU.mult)
         logs = [keep.tile([P, S], F32, name="logs%d" % j) for j in range(PACK)]
         totals = [psum.tile([P, S], F32, name="total", tag="bank%d" % j) for j in range(PACK)]
         for u in range(2):
@@ -176,7 +171,6 @@ def tile_picked_kjgaplsegspan_none_po_kernel(tc, x_words, x_scales, d_words, d_s
                     nc.vector.scalar_tensor_tensor(z2[u][:, t, :], back[:, s, :], gm_t[:, t : t + 1], b_n4[t][:, halves[u]], ALU.mult, ALU.add)
         interleave(z2_planes[0][0][:], z2[0][:])
 
-        a_win = [keep.tile([P, S], F32, name="a_win%d" % t) for t in range(PACK)]
         a_n1 = [keep.tile([P, S], F32, name="a_n1_%d" % t) for t in range(PACK)]
         z = [keep.tile([P, PACK, HALF], F32, name="z%d" % u) for u in range(2)]
         z_planes = [planes("z_%d" % u) for u in range(2)]
@@ -195,10 +189,9 @@ def tile_picked_kjgaplsegspan_none_po_kernel(tc, x_words, x_scales, d_words, d_s
         def leave_a(t):
             nc.scalar.activation(a_win[t][:], a_banks[t][:], ACT.Copy, scale=gn_neg[:, t : t + 1])
 
-        leave_a(0)
         for t in range(PACK):
-            if t + 1 < PACK:
-                leave_a(t + 1)
+            if t < 2:
+                leave_a(t + 2)
             look_up_a(t, 0)
             if t == 0:
                 quantise(*[tile[:] for tile in z2_planes[0]])
@@ -207,21 +200,20 @@ def tile_picked_kjgaplsegspan_none_po_kernel(tc, x_words, x_scales, d_words, d_s
         for t in range(PACK):
             look_up_a(t, 1)
         interleave(z_planes[0][0][:], z[0][:], nc.scalar.copy)
-        quantise(*[tile[:] for tile in z_planes[0]])
-        h_banks = [[psum.tile([P, HALF], F32, name="h_bank", tag="bank%d" % (PACK * u + t)) for t in range(PACK)] for u in range(2)]
-        for t in range(PACK):
-            add_pass(h_banks[0][t][:], 1, t, z2_planes[0], True, False)
-            add_pass(h_banks[0][t][:], 0, t, z_planes[0], False, True)
-            nc.scalar.copy(h_win[t][:, halves[0]], h_banks[0][t][:])
-        for t in range(PACK):
-            add_pass(h_banks[1][t][:], 1, t, z2_planes[1], True, False)
         interleave(z_planes[1][0][:], z[1][:])
-        quantise(*[tile[:] for tile in z_planes[1]])
+        h_banks = [[psum.tile([P, HALF], F32, name="h_bank", tag="bank%d" % (PACK * u + t)) for t in range(PACK)] for u in range(2)]
+        for u in range(2):
+            for t in range(PACK):
+                add_pass(h_banks[u][t][:], 1, t, z2_planes[u], True, False)
+        for u in range(2):
+            quantise(*[tile[:] for tile in z_planes[u]])
         for t in range(PACK):
-            add_pass(h_banks[1][t][:], 0, t, z_planes[1], False, True)
-        nc.scalar.copy(h_win[0][:, halves[1]], h_banks[1][0][:])
-        for t in range(1, PACK):
-            nc.vector.tensor_copy(h_win[t][:, halves[1]], h_banks[1][t][:])
+            for u in range(2):
+                add_pass(h_banks[u][t][:], 0, t, z_planes[u], False, True)
+        for t in range(PACK):
+            for u in range(2):
+                copy = nc.scalar.copy if t == 0 else nc.vector.tensor_copy
+                copy(h_win[t][:, halves[u]], h_banks[u][t][:])
 
         out_rows = out_0.rearrange("(p t) j -> p t j", t=PACK)
         y_codes = keep.tile([P, S], U32, name="y_codes", align_bytes=64)

@@ -15,11 +15,19 @@ ACT = mybir.ActivationFunctionType
 
 P = 128
 PACK = 4
+QUADRANTS = 4
+LINE = 4
 K, T, S, N, G, H = 512, 1024, 512, 512, 2048, 512
 HALF = S // 2
-CHUNK = 512
+MEMBERS = 4
 SPARE = 16
-FLOPS = 4 * 2 * 512 * 512 * 512
+SCORE_SCALE = 0.0625
+FLOPS = 2 * (2 * K * H * S + 2 * H * N * S)
+
+PAIRS = ((0, 1), (2, 3))
+CHUNK = S // MEMBERS
+ROUNDED_EARLY = (0, 1)
+ROUNDED_LATE = (2, 3)
 
 
 def tile_picked_kjgaplsegspan_none_po_kernel(tc, x_words, x_scales, d_words, d_scales, gn, gm, w1_words, w1_scales, w2_words, w2_scales, offs, k1, two, n1, n2, n3, n4, n5, out_0, out_1, out_2):
@@ -29,10 +37,13 @@ def tile_picked_kjgaplsegspan_none_po_kernel(tc, x_words, x_scales, d_words, d_s
         return dram[0].rearrange("p c r -> p (c r)").bitcast(I32)
 
     def deal(dst, src):
-        nc.vector.tensor_copy(out=dst.rearrange("p (t c i) -> p c t i", t=PACK, i=4), in_=src.rearrange("p (c i t) -> p c t i", t=PACK, i=4))
+        nc.vector.tensor_copy(out=dst.rearrange("p (t c i) -> p c t i", t=PACK, i=LINE), in_=src.rearrange("p (c i t) -> p c t i", t=PACK, i=LINE))
 
-    def interleave(dst, src, copy=nc.vector.tensor_copy):
-        copy(out=dst.rearrange("p (c i t) -> p c t i", i=4, t=PACK), in_=src.rearrange("p t (c i) -> p c t i", i=4))
+    def round_and_interleave(dst, src, copy=nc.vector.tensor_copy):
+        copy(out=dst.rearrange("p (c i t) -> p c t i", i=LINE, t=PACK), in_=src.rearrange("p t (c i) -> p c t i", i=LINE))
+
+    def quantise(rounded, codes, scales):
+        nc.vector.quantize_mx(out=codes.bitcast(FP8X4), scales=scales, in_=rounded)
 
     with ExitStack() as ctx:
         lists = ctx.enter_context(tc.tile_pool(name="lists", bufs=1))
@@ -53,20 +64,20 @@ def tile_picked_kjgaplsegspan_none_po_kernel(tc, x_words, x_scales, d_words, d_s
         l_k1 = load_list(k1, "l_k1")
         nc.scalar.dma_start(d_bytes[0:P:8, :].bitcast(I32), d_scales[0].bitcast(I32))
         l_two = load_list(two, "l_two")
-        for q in range(4):
+        for q in range(QUADRANTS):
             nc.scalar.dma_start(x_bytes[32 * q : 32 * q + 4, :].bitcast(I32), x_scales[0, 4 * q : 4 * q + 4, :].bitcast(I32))
-        x_tab = keep.tile([P, T], U32, name="x_tab", tag="table", align_bytes=64)
-        nc.sync.dma_start(x_tab[:].bitcast(I32), words_of(x_words))
-        l_offs = load_list(offs, "l_offs")
-        gm_t = keep.tile([P, PACK], F32, name="gm_t")
-        nc.gpsimd.dma_start(gm_t[:], gm.rearrange("(p t) o -> p (t o)", t=PACK))
-        gn_t = keep.tile([P, PACK], F32, name="gn_t")
-        nc.gpsimd.dma_start(gn_t[:], gn.rearrange("(p t) o -> p (t o)", t=PACK))
+        x_table = keep.tile([P, T], U32, name="x_table", tag="x_table", align_bytes=64)
+        nc.sync.dma_start(x_table[:].bitcast(I32), words_of(x_words))
+        l_idx = load_list(offs, "l_idx")
+        gm_rows = keep.tile([P, PACK], F32, name="gm_rows")
+        nc.gpsimd.dma_start(gm_rows[:], gm.rearrange("(p t) o -> p (t o)", t=PACK))
+        gn_rows = keep.tile([P, PACK], F32, name="gn_rows")
+        nc.gpsimd.dma_start(gn_rows[:], gn.rearrange("(p t) o -> p (t o)", t=PACK))
         l_n3 = load_list(n3, "l_n3")
         l_n4 = load_list(n4, "l_n4")
         l_n1 = load_list(n1, "l_n1")
-        d_tab = keep.tile([P, G], U32, name="d_tab", tag="dictionary", align_bytes=64)
-        nc.sync.dma_start(d_tab[:].bitcast(I32), words_of(d_words))
+        d_table = keep.tile([P, G], U32, name="d_table", tag="d_table", align_bytes=64)
+        nc.sync.dma_start(d_table[:].bitcast(I32), words_of(d_words))
         l_n2 = load_list(n2, "l_n2")
         l_n5 = load_list(n5, "l_n5")
 
@@ -76,192 +87,198 @@ def tile_picked_kjgaplsegspan_none_po_kernel(tc, x_words, x_scales, d_words, d_s
             return picked
 
         key_scales = keep.tile([P, H], U8, name="key_scales", align_bytes=64)
-        key_bytes = pick(d_bytes, l_k1, U8, "key_bytes", "picked_first")
+        key_bytes = pick(d_bytes, l_k1, U8, "key_bytes", "picked")
         deal(key_scales[:], key_bytes[:])
         for r, queue in ((1, nc.scalar), (2, nc.sync), (3, nc.sync)):
             queue.dma_start(key_scales[r:P:32, :].bitcast(I32), key_scales[8 * r : P : 32, :].bitcast(I32))
         two_scales = pick(x_bytes, l_two, U8, "two_scales", "d_bytes")
-        two_codes = pick(x_tab, l_two, U32, "two_codes", "two_codes")
-        key_words = pick(d_tab, l_k1, U32, "key_words", "picked_first")
+        two_codes = pick(x_table, l_two, U32, "two_codes", "two_codes")
+        key_words = pick(d_table, l_k1, U32, "key_words", "picked")
         key_codes = keep.tile([P, H], U32, name="key_codes", align_bytes=64)
         deal(key_codes[:], key_words[:])
 
-        def score(t, codes, scales, tag):
-            bank = psum.tile([P, S], F32, name="bank", tag=tag)
-            cols = slice(P * t, P * (t + 1))
-            nc.tensor.matmul_mx(out=bank[:], lhsT=key_codes[:, cols].bitcast(FP8X4), lhsT_scale=key_scales[:, cols],
-                                rhs=codes[:].bitcast(FP8X4), rhs_scale=scales, start=True, stop=True)
-            return bank
+        halves = [slice(HALF * u, HALF * (u + 1)) for u in range(2)]
+        blocks = [slice(P * j, P * (j + 1)) for j in range(PACK)]
 
-        b_banks = [score(t, two_codes, two_scales[:], "bank%d" % t) for t in range(PACK)]
-        idx_scales = pick(x_bytes, l_offs, U8, "idx_scales", "picked_first")
-        idx_codes = pick(x_tab, l_offs, U32, "idx_codes", "dictionary")
-        a_banks = [score(t, idx_codes, idx_scales[:], "bank%d" % (PACK + t)) for t in range(PACK)]
+        def score(t, codes, scales, bank):
+            out = psum.tile([P, S], F32, name="score", tag="bank%d" % bank)
+            nc.tensor.matmul_mx(out=out[:], lhsT=key_codes[:, blocks[t]].bitcast(FP8X4), lhsT_scale=key_scales[:, blocks[t]],
+                                rhs=codes[:].bitcast(FP8X4), rhs_scale=scales[:], start=True, stop=True)
+            return out
 
-        gm_neg = keep.tile([P, PACK], F32, name="gm_neg")
-        nc.gpsimd.tensor_scalar(gm_neg[:], gm_t[:], -0.0625, None, ALU.mult)
-        gn_neg = keep.tile([P, PACK], F32, name="gn_neg")
-        nc.gpsimd.tensor_scalar(gn_neg[:], gn_t[:], -0.0625, None, ALU.mult)
+        b_banks = [score(t, two_codes, two_scales, t) for t in range(PACK)]
+        idx_scales = pick(x_bytes, l_idx, U8, "idx_scales", "picked")
+        idx_codes = pick(x_table, l_idx, U32, "idx_codes", "d_table")
+        a_banks = [score(t, idx_codes, idx_scales, PACK + t) for t in range(PACK)]
 
-        w_tab = keep.tile([P, 2, N], U32, name="w_tab", tag="table", align_bytes=64)
+        b_factor = keep.tile([P, PACK], F32, name="b_factor")
+        nc.gpsimd.tensor_scalar(b_factor[:], gm_rows[:], -SCORE_SCALE, None, ALU.mult)
+        a_factor = keep.tile([P, PACK], F32, name="a_factor")
+        nc.gpsimd.tensor_scalar(a_factor[:], gn_rows[:], -SCORE_SCALE, None, ALU.mult)
+
+        w_table = keep.tile([P, 2, N], U32, name="w_table", tag="x_table", align_bytes=64)
         w_bytes = keep.tile([P, N], U8, name="w_bytes", tag="x_bytes", align_bytes=64)
         nc.gpsimd.memset(w_bytes[:].bitcast(I32), 0)
         identity = keep.tile([P, P], F32, name="identity")
         make_identity(nc, identity[:])
-        nc.sync.dma_start(w_tab[:, 0, :].bitcast(I32), words_of(w1_words))
-        nc.sync.dma_start(w_tab[:, 1, :].bitcast(I32), words_of(w2_words))
+        nc.sync.dma_start(w_table[:, 0, :].bitcast(I32), words_of(w1_words))
+        nc.sync.dma_start(w_table[:, 1, :].bitcast(I32), words_of(w2_words))
         for w, scales in enumerate((w1_scales, w2_scales)):
-            for q in range(4):
+            for q in range(QUADRANTS):
                 nc.sync.dma_start(w_bytes[32 * q + 4 * w : 32 * q + 4 * w + 4, :].bitcast(I32), scales[0, 4 * q : 4 * q + 4, :].bitcast(I32))
 
         def half_of(offsets, u):
-            return offsets[:, 16 * u : 16 * (u + 1)]
+            return offsets[:, HALF // 16 * u : HALF // 16 * (u + 1)]
 
-        halves = [slice(HALF * u, HALF * (u + 1)) for u in range(2)]
-        blocks = [slice(P * j, P * (j + 1)) for j in range(PACK)]
-        ex = [keep.tile([P, S], F32, name="ex%d" % t) for t in range(PACK)]
-        b_win = [keep.tile([P, S], F32, name="b_win%d" % t) for t in range(PACK)]
-        ex_n3 = [keep.tile([P, S], F32, name="ex_n3_%d" % t) for t in range(PACK)]
-        b_n4 = [keep.tile([P, S], F32, name="b_n4_%d" % t) for t in range(PACK)]
+        def row_tiles(name):
+            return [keep.tile([P, S], F32, name="%s%d" % (name, t)) for t in range(PACK)]
+
+        ex, b_window, ex_n3, b_n4 = row_tiles("ex"), row_tiles("b_window"), row_tiles("ex_n3"), row_tiles("b_n4")
         for t in range(PACK):
-            nc.scalar.activation(ex[t][:], b_banks[t][:], ACT.Exp, scale=0.0625)
-            nc.vector.tensor_scalar(b_win[t][:], b_banks[t][:], gm_neg[:, t : t + 1], None, ALU.mult)
+            nc.scalar.activation(ex[t][:], b_banks[t][:], ACT.Exp, scale=SCORE_SCALE)
+            nc.vector.tensor_scalar(b_window[t][:], b_banks[t][:], b_factor[:, t : t + 1], None, ALU.mult)
         for u in range(2):
             for t in range(PACK):
                 nc.scalar.activation(ex_n3[t][:, halves[u]], ex[t][:].indirect(half_of(l_n3, u)), ACT.Copy)
-                nc.vector.tensor_copy(b_n4[t][:, halves[u]], b_win[t][:].indirect(half_of(l_n4, u)))
+                nc.vector.tensor_copy(b_n4[t][:, halves[u]], b_window[t][:].indirect(half_of(l_n4, u)))
         w_codes = keep.tile([P, 2, N], U32, name="w_codes", align_bytes=64)
         for w in range(2):
-            deal(w_codes[:, w, :], w_tab[:, w, :])
+            deal(w_codes[:, w, :], w_table[:, w, :])
         w_scales = keep.tile([P, N], U8, name="w_scales", align_bytes=64)
         deal(w_scales[:], w_bytes[:])
 
-        a_win = [keep.tile([P, S], F32, name="a_win%d" % t) for t in range(PACK)]
-        for t in range(2):
-            nc.vector.tensor_scalar(a_win[t][:], a_banks[t][:], gn_neg[:, t : t + 1], None, ALU.mult)
-        logs = [keep.tile([P, S], F32, name="logs%d" % j) for j in range(PACK)]
-        totals = [psum.tile([P, S], F32, name="total", tag="bank%d" % j) for j in range(PACK)]
+        a_window = row_tiles("a_window")
+        for t in (0, 1):
+            nc.vector.tensor_scalar(a_window[t][:], a_banks[t][:], a_factor[:, t : t + 1], None, ALU.mult)
+
+        logs_turned = row_tiles("logs_turned")
+        sums_turned = [psum.tile([P, S], F32, name="sums_turned", tag="bank%d" % j) for j in range(PACK)]
         for u in range(2):
             for t in range(PACK):
                 for j in (2 * u, 2 * u + 1):
-                    nc.tensor.matmul(totals[j][:, blocks[t]], ex[t][:, blocks[j]], identity[:], start=True, stop=False, is_transpose=True)
-                    nc.tensor.matmul(totals[j][:, blocks[t]], ex_n3[t][:, blocks[j]], identity[:], start=False, stop=True, is_transpose=True)
+                    nc.tensor.matmul(sums_turned[j][:, blocks[t]], ex[t][:, blocks[j]], identity[:], start=True, stop=False, is_transpose=True)
+                    nc.tensor.matmul(sums_turned[j][:, blocks[t]], ex_n3[t][:, blocks[j]], identity[:], start=False, stop=True, is_transpose=True)
         for j in range(PACK):
-            nc.scalar.activation(logs[j][:], totals[j][:], ACT.Ln)
+            nc.scalar.activation(logs_turned[j][:], sums_turned[j][:], ACT.Ln)
 
-        def planes(name):
-            rounded = keep.tile([P, PACK * HALF], BF16, name=name + "_round", align_bytes=64)
+        def operand(name):
+            rounded = keep.tile([P, PACK * HALF], BF16, name=name + "_rounded", align_bytes=64)
             codes = keep.tile([P, HALF], U32, name=name + "_codes", align_bytes=64)
             scales = keep.tile([P, HALF], U8, name=name + "_scales", align_bytes=64)
-            return rounded, codes, scales
-
-        def quantise(rounded, codes, scales):
-            nc.vector.quantize_mx(out=codes.bitcast(FP8X4), scales=scales, in_=rounded)
+            return rounded[:], codes[:], scales[:]
 
         z2 = [keep.tile([P, PACK, HALF], F32, name="z2_%d" % u) for u in range(2)]
-        z2_planes = [planes("z2_%d" % u) for u in range(2)]
+        z2_operand = [operand("z2_%d" % u) for u in range(2)]
         for u in range(2):
-            for pair in range(2):
-                back = psum.tile([P, 2, HALF], F32, name="back", tag="bank%d" % (2 * u + pair))
-                for s in range(2):
+            for number, pair in enumerate(PAIRS):
+                logs = psum.tile([P, 2, HALF], F32, name="logs", tag="bank%d" % (2 * u + number))
+                for s, t in enumerate(pair):
                     for i in range(2):
-                        nc.tensor.transpose(back[:, s, blocks[i]], logs[2 * u + i][:, blocks[2 * pair + s]], identity[:])
-                for s in range(2):
-                    t = 2 * pair + s
-                    nc.vector.scalar_tensor_tensor(z2[u][:, t, :], back[:, s, :], gm_t[:, t : t + 1], b_n4[t][:, halves[u]], ALU.mult, ALU.add)
-        interleave(z2_planes[0][0][:], z2[0][:])
+                        nc.tensor.transpose(logs[:, s, blocks[i]], logs_turned[2 * u + i][:, blocks[t]], identity[:])
+                for s, t in enumerate(pair):
+                    nc.vector.scalar_tensor_tensor(z2[u][:, t, :], logs[:, s, :], gm_rows[:, t : t + 1], b_n4[t][:, halves[u]], ALU.mult, ALU.add)
 
-        a_n1 = [keep.tile([P, S], F32, name="a_n1_%d" % t) for t in range(PACK)]
+        a_n1 = row_tiles("a_n1")
         z = [keep.tile([P, PACK, HALF], F32, name="z%d" % u) for u in range(2)]
-        z_planes = [planes("z_%d" % u) for u in range(2)]
-        h_win = [keep.tile([P, S + SPARE], F32, name="h_win%d" % t) for t in range(PACK)]
+        z_operand = [operand("z_%d" % u) for u in range(2)]
+        h_window = [keep.tile([P, S + SPARE], F32, name="h_window%d" % t) for t in range(PACK)]
         for t in range(PACK):
-            nc.gpsimd.memset(h_win[t][:, S:], 0.0)
+            nc.gpsimd.memset(h_window[t][:, S:], 0.0)
 
         def look_up_a(t, u):
-            nc.scalar.activation(a_n1[t][:, halves[u]], a_win[t][:].indirect(half_of(l_n1, u)), ACT.Copy)
-            nc.vector.tensor_tensor(z[u][:, t, :], a_win[t][:].indirect(half_of(l_n2, u)), a_n1[t][:, halves[u]], ALU.subtract)
-
-        def add_pass(out, w, t, operand, start, stop):
-            nc.tensor.matmul_mx(out=out, lhsT=w_codes[:, w, blocks[t]].bitcast(FP8X4), lhsT_scale=w_scales[4 * w : P, blocks[t]],
-                                rhs=operand[1][:].bitcast(FP8X4), rhs_scale=operand[2][:], start=start, stop=stop)
+            nc.scalar.activation(a_n1[t][:, halves[u]], a_window[t][:].indirect(half_of(l_n1, u)), ACT.Copy)
+            nc.vector.tensor_tensor(z[u][:, t, :], a_window[t][:].indirect(half_of(l_n2, u)), a_n1[t][:, halves[u]], ALU.subtract)
 
         def leave_a(t):
-            nc.scalar.activation(a_win[t][:], a_banks[t][:], ACT.Copy, scale=gn_neg[:, t : t + 1])
+            nc.scalar.activation(a_window[t][:], a_banks[t][:], ACT.Copy, scale=a_factor[:, t : t + 1])
 
-        for t in range(PACK):
-            if t < 2:
-                leave_a(t + 2)
-            look_up_a(t, 0)
-            if t == 0:
-                quantise(*[tile[:] for tile in z2_planes[0]])
-        interleave(z2_planes[1][0][:], z2[1][:], nc.scalar.copy)
-        quantise(*[tile[:] for tile in z2_planes[1]])
+        leave_a(2)
+        look_up_a(0, 0)
+        leave_a(3)
+        look_up_a(1, 0)
+        round_and_interleave(z2_operand[0][0], z2[0][:], nc.scalar.copy)
+        look_up_a(2, 0)
+        quantise(*z2_operand[0])
+        look_up_a(3, 0)
+        round_and_interleave(z2_operand[1][0], z2[1][:], nc.scalar.copy)
+        quantise(*z2_operand[1])
         for t in range(PACK):
             look_up_a(t, 1)
-        interleave(z_planes[0][0][:], z[0][:], nc.scalar.copy)
-        interleave(z_planes[1][0][:], z[1][:])
+        round_and_interleave(z_operand[0][0], z[0][:], nc.scalar.copy)
+        round_and_interleave(z_operand[1][0], z[1][:])
+
+        def add_pass(out, w, t, moving, opens):
+            rounded, codes, scales = moving
+            nc.tensor.matmul_mx(out=out[:], lhsT=w_codes[:, w, blocks[t]].bitcast(FP8X4), lhsT_scale=w_scales[4 * w : P, blocks[t]],
+                                rhs=codes.bitcast(FP8X4), rhs_scale=scales, start=opens, stop=not opens)
+
         h_banks = [[psum.tile([P, HALF], F32, name="h_bank", tag="bank%d" % (PACK * u + t)) for t in range(PACK)] for u in range(2)]
         for u in range(2):
             for t in range(PACK):
-                add_pass(h_banks[u][t][:], 1, t, z2_planes[u], True, False)
+                add_pass(h_banks[u][t], 1, t, z2_operand[u], True)
         for u in range(2):
-            quantise(*[tile[:] for tile in z_planes[u]])
+            quantise(*z_operand[u])
         for t in range(PACK):
             for u in range(2):
-                add_pass(h_banks[u][t][:], 0, t, z_planes[u], False, True)
+                add_pass(h_banks[u][t], 0, t, z_operand[u], False)
         for t in range(PACK):
             for u in range(2):
                 copy = nc.scalar.copy if t == 0 else nc.vector.tensor_copy
-                copy(h_win[t][:, halves[u]], h_banks[u][t][:])
+                copy(h_window[t][:, halves[u]], h_banks[u][t][:])
 
+        chunks = [(first, CHUNK, PAIRS) for first in range(0, S - CHUNK, CHUNK)]
+        chunks.append((S - CHUNK, CHUNK // 2, PAIRS))
+        chunks.append((S - CHUNK // 2, CHUNK // 2, ((0, 1), (2,), (3,))))
         out_rows = out_0.rearrange("(p t) j -> p t j", t=PACK)
         y_codes = keep.tile([P, S], U32, name="y_codes", align_bytes=64)
         y_scales = keep.tile([P, S], U8, name="y_scales", align_bytes=64)
         out_words = words_of(out_1)
-        chunks = [(0, 128, ((0, 1), (2, 3))), (128, 128, ((0, 1), (2, 3))), (256, 128, ((0, 1), (2, 3))),
-                  (384, 64, ((0, 1), (2, 3))), (448, 64, ((0, 1), (2,), (3,)))]
         y = [keep.tile([P, PACK, places], F32, name="y%d" % c) for c, (first, places, groups) in enumerate(chunks)]
-        y_round = [keep.tile([P, PACK * places], BF16, name="y_round%d" % c, align_bytes=64) for c, (first, places, groups) in enumerate(chunks)]
+        y_rounded = [keep.tile([P, PACK * places], BF16, name="y_rounded%d" % c, align_bytes=64) for c, (first, places, groups) in enumerate(chunks)]
 
-        def combine(c, group, mx, mn):
+        def combine(c, group, largest, smallest):
             first, places, groups = chunks[c]
-            nc.vector.scalar_tensor_tensor(y[c][:, group[0] : group[-1] + 1, :].rearrange("p s j -> p (s j)"), mn[:], -0.5, mx[:], ALU.mult, ALU.add)
+            nc.vector.scalar_tensor_tensor(y[c][:, group[0] : group[-1] + 1, :].rearrange("p s j -> p (s j)"), smallest[:], -0.5, largest[:], ALU.mult, ALU.add)
             if group == groups[-1]:
                 nc.sync.dma_start(out_rows[:, :, first : first + places], y[c][:])
 
         def store_codes(c):
             first, places, groups = chunks[c]
             cols = slice(first, first + places)
-            quantise(y_round[c][:], y_codes[:, cols], y_scales[:, cols])
+            quantise(y_rounded[c][:], y_codes[:, cols], y_scales[:, cols])
             nc.sync.dma_start(out_words[:, cols], y_codes[:, cols].bitcast(I32))
 
-        waiting = None
+        uncombined = None
         for c, (first, places, groups) in enumerate(chunks):
+            entries = l_n5[:, MEMBERS * first // 16 : MEMBERS * (first + places) // 16]
             for number, group in enumerate(groups):
                 width = len(group) * places
-                members = ring.tile([P, len(group), 4 * places], F32, name="members")
+                members = ring.tile([P, len(group), MEMBERS * places], F32, name="members")
                 for s, t in enumerate(group):
-                    nc.scalar.activation(members[:, s, :], h_win[t][:].indirect(l_n5[:, first // 4 : (first + places) // 4]), ACT.Copy)
-                four = members[:].rearrange("p s (j e) -> p (s j) e", e=4)
+                    nc.scalar.activation(members[:, s, :], h_window[t][:].indirect(entries), ACT.Copy)
+                four = members[:].rearrange("p s (j e) -> p (s j) e", e=MEMBERS)
                 high = ring.tile([P, width, 2], F32, name="high")
                 low = ring.tile([P, width, 2], F32, name="low")
-                mx = ring.tile([P, width], F32, name="mx")
-                mn = ring.tile([P, width], F32, name="mn")
+                largest = ring.tile([P, width], F32, name="largest")
+                smallest = ring.tile([P, width], F32, name="smallest")
                 nc.vector.tensor_tensor(high[:], four[:, :, 0:2], four[:, :, 2:4], ALU.max)
-                if waiting is not None:
-                    combine(*waiting)
+                if uncombined is not None:
+                    combine(*uncombined)
                 nc.vector.tensor_tensor(low[:], four[:, :, 0:2], four[:, :, 2:4], ALU.min)
-                nc.vector.tensor_tensor(mx[:], high[:, :, 0], high[:, :, 1], ALU.max)
-                if c > 0 and number == 0:
-                    interleave(y_round[c - 1][:], y[c - 1][:])
-                if c > 0 and number == 1:
+                nc.vector.tensor_tensor(largest[:], high[:, :, 0], high[:, :, 1], ALU.max)
+                if c - 1 in ROUNDED_EARLY and number == 0:
+                    round_and_interleave(y_rounded[c - 1][:], y[c - 1][:])
+                if c - 1 in ROUNDED_EARLY and number == 1:
                     store_codes(c - 1)
-                nc.vector.tensor_tensor(mn[:], low[:, :, 0], low[:, :, 1], ALU.min)
-                waiting = (c, group, mx, mn)
-        combine(*waiting)
-        interleave(y_round[len(chunks) - 1][:], y[len(chunks) - 1][:])
-        store_codes(len(chunks) - 1)
-        for q in range(4):
+                nc.vector.tensor_tensor(smallest[:], low[:, :, 0], low[:, :, 1], ALU.min)
+                uncombined = (c, group, largest, smallest)
+        for c in ROUNDED_LATE:
+            round_and_interleave(y_rounded[c][:], y[c][:], nc.scalar.copy)
+            store_codes(c)
+        last = len(chunks) - 1
+        combine(*uncombined)
+        round_and_interleave(y_rounded[last][:], y[last][:])
+        store_codes(last)
+        for q in range(QUADRANTS):
             queue = nc.sync if q % 2 == 0 else nc.scalar
             queue.dma_start(out_2[0, 4 * q : 4 * q + 4, :].bitcast(I32), y_scales[32 * q : 32 * q + 4, :].bitcast(I32))

from contextlib import ExitStack

import concourse.mybir as mybir
from concourse.masks import make_identity

F32 = mybir.dt.float32
BF16 = mybir.dt.bfloat16
I32 = mybir.dt.int32
U32 = mybir.dt.uint32
U16 = mybir.dt.uint16
U8 = mybir.dt.uint8
FP8X4 = mybir.dt.float8_e4m3fn_x4
ALU = mybir.AluOpType
ACT = mybir.ActivationFunctionType

P = 128
PACK = 4
QUADRANTS = 4
LINE = 4
K, T, S, N, G, H = 512, 1024, 512, 512, 2048, 512
HALF = S // 2
MEMBERS = 4
SPARE = 16
SCORE_SCALE = 0.0625
FLOPS = 2 * (2 * K * H * S + 2 * H * N * S)

PAIRS = ((0, 1), (2, 3))
CHUNK = S // MEMBERS
ROUNDED_EARLY = (0, 1)
ROUNDED_LATE = (2, 3)


def tile_picked_kjgaplsegspan_none_po_kernel(tc, x_words, x_scales, d_words, d_scales, gn, gm, w1_words, w1_scales, w2_words, w2_scales, offs, k1, two, n1, n2, n3, n4, n5, out_0, out_1, out_2):
    nc = tc.nc

    def words_of(dram):
        return dram[0].rearrange("p c r -> p (c r)").bitcast(I32)

    def deal(dst, src):
        nc.vector.tensor_copy(out=dst.rearrange("p (t c i) -> p c t i", t=PACK, i=LINE), in_=src.rearrange("p (c i t) -> p c t i", t=PACK, i=LINE))

    def round_and_interleave(dst, src, copy=nc.vector.tensor_copy):
        copy(out=dst.rearrange("p (c i t) -> p c t i", i=LINE, t=PACK), in_=src.rearrange("p t (c i) -> p c t i", i=LINE))

    def quantise(rounded, codes, scales):
        nc.vector.quantize_mx(out=codes.bitcast(FP8X4), scales=scales, in_=rounded)

    with ExitStack() as ctx:
        lists = ctx.enter_context(tc.tile_pool(name="lists", bufs=1))
        keep = ctx.enter_context(tc.tile_pool(name="keep", bufs=1))
        ring = ctx.enter_context(tc.tile_pool(name="ring", bufs=3))
        psum = ctx.enter_context(tc.psum_pool(name="psum", bufs=1))

        def load_list(dram, name):
            tile = lists.tile(list(dram.shape), U16, name=name)
            nc.sync.dma_start(tile[:], dram)
            return tile

        d_bytes = keep.tile([P, G], U8, name="d_bytes", tag="d_bytes", align_bytes=64)
        x_bytes = keep.tile([P, T], U8, name="x_bytes", tag="x_bytes", align_bytes=64)
        nc.vector.memset(d_bytes[:].bitcast(I32), 0)
        nc.vector.memset(x_bytes[:].bitcast(I32), 0)

        l_k1 = load_list(k1, "l_k1")
        nc.scalar.dma_start(d_bytes[0:P:8, :].bitcast(I32), d_scales[0].bitcast(I32))
        l_two = load_list(two, "l_two")
        for q in range(QUADRANTS):
            nc.scalar.dma_start(x_bytes[32 * q : 32 * q + 4, :].bitcast(I32), x_scales[0, 4 * q : 4 * q + 4, :].bitcast(I32))
        x_table = keep.tile([P, T], U32, name="x_table", tag="x_table", align_bytes=64)
        nc.sync.dma_start(x_table[:].bitcast(I32), words_of(x_words))
        l_idx = load_list(offs, "l_idx")
        gm_rows = keep.tile([P, PACK], F32, name="gm_rows")
        nc.gpsimd.dma_start(gm_rows[:], gm.rearrange("(p t) o -> p (t o)", t=PACK))
        gn_rows = keep.tile([P, PACK], F32, name="gn_rows")
        nc.gpsimd.dma_start(gn_rows[:], gn.rearrange("(p t) o -> p (t o)", t=PACK))
        l_n3 = load_list(n3, "l_n3")
        l_n4 = load_list(n4, "l_n4")
        l_n1 = load_list(n1, "l_n1")
        d_table = keep.tile([P, G], U32, name="d_table", tag="d_table", align_bytes=64)
        nc.sync.dma_start(d_table[:].bitcast(I32), words_of(d_words))
        l_n2 = load_list(n2, "l_n2")
        l_n5 = load_list(n5, "l_n5")

        def pick(table, offsets, dtype, name, tag):
            picked = keep.tile([P, S], dtype, name=name, tag=tag, align_bytes=64)
            nc.vector.tensor_copy(picked[:], table[:].indirect(offsets[:]))
            return picked

        key_scales = keep.tile([P, H], U8, name="key_scales", align_bytes=64)
        key_bytes = pick(d_bytes, l_k1, U8, "key_bytes", "picked")
        deal(key_scales[:], key_bytes[:])
        for r, queue in ((1, nc.scalar), (2, nc.sync), (3, nc.sync)):
            queue.dma_start(key_scales[r:P:32, :].bitcast(I32), key_scales[8 * r : P : 32, :].bitcast(I32))
        two_scales = pick(x_bytes, l_two, U8, "two_scales", "d_bytes")
        two_codes = pick(x_table, l_two, U32, "two_codes", "two_codes")
        key_words = pick(d_table, l_k1, U32, "key_words", "picked")
        key_codes = keep.tile([P, H], U32, name="key_codes", align_bytes=64)
        deal(key_codes[:], key_words[:])

        halves = [slice(HALF * u, HALF * (u + 1)) for u in range(2)]
        blocks = [slice(P * j, P * (j + 1)) for j in range(PACK)]

        def score(t, codes, scales, bank):
            out = psum.tile([P, S], F32, name="score", tag="bank%d" % bank)
            nc.tensor.matmul_mx(out=out[:], lhsT=key_codes[:, blocks[t]].bitcast(FP8X4), lhsT_scale=key_scales[:, blocks[t]],
                                rhs=codes[:].bitcast(FP8X4), rhs_scale=scales[:], start=True, stop=True)
            return out

        b_banks = [score(t, two_codes, two_scales, t) for t in range(PACK)]
        idx_scales = pick(x_bytes, l_idx, U8, "idx_scales", "picked")
        idx_codes = pick(x_table, l_idx, U32, "idx_codes", "d_table")
        a_banks = [score(t, idx_codes, idx_scales, PACK + t) for t in range(PACK)]

        b_factor = keep.tile([P, PACK], F32, name="b_factor")
        nc.gpsimd.tensor_scalar(b_factor[:], gm_rows[:], -SCORE_SCALE, None, ALU.mult)
        a_factor = keep.tile([P, PACK], F32, name="a_factor")
        nc.gpsimd.tensor_scalar(a_factor[:], gn_rows[:], -SCORE_SCALE, None, ALU.mult)

        w_table = keep.tile([P, 2, N], U32, name="w_table", tag="x_table", align_bytes=64)
        w_bytes = keep.tile([P, N], U8, name="w_bytes", tag="x_bytes", align_bytes=64)
        nc.gpsimd.memset(w_bytes[:].bitcast(I32), 0)
        identity = keep.tile([P, P], F32, name="identity")
        make_identity(nc, identity[:])
        nc.sync.dma_start(w_table[:, 0, :].bitcast(I32), words_of(w1_words))
        nc.sync.dma_start(w_table[:, 1, :].bitcast(I32), words_of(w2_words))
        for w, scales in enumerate((w1_scales, w2_scales)):
            for q in range(QUADRANTS):
                nc.sync.dma_start(w_bytes[32 * q + 4 * w : 32 * q + 4 * w + 4, :].bitcast(I32), scales[0, 4 * q : 4 * q + 4, :].bitcast(I32))

        def half_of(offsets, u):
            return offsets[:, HALF // 16 * u : HALF // 16 * (u + 1)]

        def row_tiles(name):
            return [keep.tile([P, S], F32, name="%s%d" % (name, t)) for t in range(PACK)]

        ex, b_window, ex_n3, b_n4 = row_tiles("ex"), row_tiles("b_window"), row_tiles("ex_n3"), row_tiles("b_n4")
        for t in range(PACK):
            nc.scalar.activation(ex[t][:], b_banks[t][:], ACT.Exp, scale=SCORE_SCALE)
            nc.vector.tensor_scalar(b_window[t][:], b_banks[t][:], b_factor[:, t : t + 1], None, ALU.mult)
        for u in range(2):
            for t in range(PACK):
                nc.scalar.activation(ex_n3[t][:, halves[u]], ex[t][:].indirect(half_of(l_n3, u)), ACT.Copy)
                nc.vector.tensor_copy(b_n4[t][:, halves[u]], b_window[t][:].indirect(half_of(l_n4, u)))
        w_codes = keep.tile([P, 2, N], U32, name="w_codes", align_bytes=64)
        for w in range(2):
            deal(w_codes[:, w, :], w_table[:, w, :])
        w_scales = keep.tile([P, N], U8, name="w_scales", align_bytes=64)
        deal(w_scales[:], w_bytes[:])

        a_window = row_tiles("a_window")
        for t in (0, 1):
            nc.vector.tensor_scalar(a_window[t][:], a_banks[t][:], a_factor[:, t : t + 1], None, ALU.mult)

        logs_turned = row_tiles("logs_turned")
        sums_turned = [psum.tile([P, S], F32, name="sums_turned", tag="bank%d" % j) for j in range(PACK)]
        for u in range(2):
            for t in range(PACK):
                for j in (2 * u, 2 * u + 1):
                    nc.tensor.matmul(sums_turned[j][:, blocks[t]], ex[t][:, blocks[j]], identity[:], start=True, stop=False, is_transpose=True)
                    nc.tensor.matmul(sums_turned[j][:, blocks[t]], ex_n3[t][:, blocks[j]], identity[:], start=False, stop=True, is_transpose=True)
        for j in range(PACK):
            nc.scalar.activation(logs_turned[j][:], sums_turned[j][:], ACT.Ln)

        def operand(name):
            rounded = keep.tile([P, PACK * HALF], BF16, name=name + "_rounded", align_bytes=64)
            codes = keep.tile([P, HALF], U32, name=name + "_codes", align_bytes=64)
            scales = keep.tile([P, HALF], U8, name=name + "_scales", align_bytes=64)
            return rounded[:], codes[:], scales[:]

        z2 = [keep.tile([P, PACK, HALF], F32, name="z2_%d" % u) for u in range(2)]
        z2_operand = [operand("z2_%d" % u) for u in range(2)]
        for u in range(2):
            for number, pair in enumerate(PAIRS):
                logs = psum.tile([P, 2, HALF], F32, name="logs", tag="bank%d" % (2 * u + number))
                for s, t in enumerate(pair):
                    for i in range(2):
                        nc.tensor.transpose(logs[:, s, blocks[i]], logs_turned[2 * u + i][:, blocks[t]], identity[:])
                for s, t in enumerate(pair):
                    nc.vector.scalar_tensor_tensor(z2[u][:, t, :], logs[:, s, :], gm_rows[:, t : t + 1], b_n4[t][:, halves[u]], ALU.mult, ALU.add)

        a_n1 = row_tiles("a_n1")
        z = [keep.tile([P, PACK, HALF], F32, name="z%d" % u) for u in range(2)]
        z_operand = [operand("z_%d" % u) for u in range(2)]
        h_window = [keep.tile([P, S + SPARE], F32, name="h_window%d" % t) for t in range(PACK)]
        for t in range(PACK):
            nc.gpsimd.memset(h_window[t][:, S:], 0.0)

        def look_up_a(t, u):
            nc.scalar.activation(a_n1[t][:, halves[u]], a_window[t][:].indirect(half_of(l_n1, u)), ACT.Copy)
            nc.vector.tensor_tensor(z[u][:, t, :], a_window[t][:].indirect(half_of(l_n2, u)), a_n1[t][:, halves[u]], ALU.subtract)

        def leave_a(t):
            nc.scalar.activation(a_window[t][:], a_banks[t][:], ACT.Copy, scale=a_factor[:, t : t + 1])

        leave_a(2)
        look_up_a(0, 0)
        leave_a(3)
        look_up_a(1, 0)
        round_and_interleave(z2_operand[0][0], z2[0][:], nc.scalar.copy)
        look_up_a(2, 0)
        quantise(*z2_operand[0])
        look_up_a(3, 0)
        round_and_interleave(z2_operand[1][0], z2[1][:], nc.scalar.copy)
        quantise(*z2_operand[1])
        for t in range(PACK):
            look_up_a(t, 1)
        round_and_interleave(z_operand[0][0], z[0][:], nc.scalar.copy)
        round_and_interleave(z_operand[1][0], z[1][:])

        def add_pass(out, w, t, moving, opens):
            rounded, codes, scales = moving
            nc.tensor.matmul_mx(out=out[:], lhsT=w_codes[:, w, blocks[t]].bitcast(FP8X4), lhsT_scale=w_scales[4 * w : P, blocks[t]],
                                rhs=codes.bitcast(FP8X4), rhs_scale=scales, start=opens, stop=not opens)

        h_banks = [[psum.tile([P, HALF], F32, name="h_bank", tag="bank%d" % (PACK * u + t)) for t in range(PACK)] for u in range(2)]
        for u in range(2):
            for t in range(PACK):
                add_pass(h_banks[u][t], 1, t, z2_operand[u], True)
        for u in range(2):
            quantise(*z_operand[u])
        for t in range(PACK):
            for u in range(2):
                add_pass(h_banks[u][t], 0, t, z_operand[u], False)
        for t in range(PACK):
            for u in range(2):
                copy = nc.scalar.copy if t == 0 else nc.vector.tensor_copy
                copy(h_window[t][:, halves[u]], h_banks[u][t][:])

        chunks = [(first, CHUNK, PAIRS) for first in range(0, S - CHUNK, CHUNK)]
        chunks.append((S - CHUNK, CHUNK // 2, PAIRS))
        chunks.append((S - CHUNK // 2, CHUNK // 2, ((0, 1), (2,), (3,))))
        out_rows = out_0.rearrange("(p t) j -> p t j", t=PACK)
        y_codes = keep.tile([P, S], U32, name="y_codes", align_bytes=64)
        y_scales = keep.tile([P, S], U8, name="y_scales", align_bytes=64)
        out_words = words_of(out_1)
        y = [keep.tile([P, PACK, places], F32, name="y%d" % c) for c, (first, places, groups) in enumerate(chunks)]
        y_rounded = [keep.tile([P, PACK * places], BF16, name="y_rounded%d" % c, align_bytes=64) for c, (first, places, groups) in enumerate(chunks)]

        def combine(c, group, largest, smallest):
            first, places, groups = chunks[c]
            nc.vector.scalar_tensor_tensor(y[c][:, group[0] : group[-1] + 1, :].rearrange("p s j -> p (s j)"), smallest[:], -0.5, largest[:], ALU.mult, ALU.add)
            if group == groups[-1]:
                nc.sync.dma_start(out_rows[:, :, first : first + places], y[c][:])

        def store_codes(c):
            first, places, groups = chunks[c]
            cols = slice(first, first + places)
            quantise(y_rounded[c][:], y_codes[:, cols], y_scales[:, cols])
            nc.sync.dma_start(out_words[:, cols], y_codes[:, cols].bitcast(I32))

        uncombined = None
        for c, (first, places, groups) in enumerate(chunks):
            entries = l_n5[:, MEMBERS * first // 16 : MEMBERS * (first + places) // 16]
            for number, group in enumerate(groups):
                width = len(group) * places
                members = ring.tile([P, len(group), MEMBERS * places], F32, name="members")
                for s, t in enumerate(group):
                    nc.scalar.activation(members[:, s, :], h_window[t][:].indirect(entries), ACT.Copy)
                four = members[:].rearrange("p s (j e) -> p (s j) e", e=MEMBERS)
                high = ring.tile([P, width, 2], F32, name="high")
                low = ring.tile([P, width, 2], F32, name="low")
                largest = ring.tile([P, width], F32, name="largest")
                smallest = ring.tile([P, width], F32, name="smallest")
                nc.vector.tensor_tensor(high[:], four[:, :, 0:2], four[:, :, 2:4], ALU.max)
                if uncombined is not None:
                    combine(*uncombined)
                nc.vector.tensor_tensor(low[:], four[:, :, 0:2], four[:, :, 2:4], ALU.min)
                nc.vector.tensor_tensor(largest[:], high[:, :, 0], high[:, :, 1], ALU.max)
                if c - 1 in ROUNDED_EARLY and number == 0:
                    round_and_interleave(y_rounded[c - 1][:], y[c - 1][:])
                if c - 1 in ROUNDED_EARLY and number == 1:
                    store_codes(c - 1)
                nc.vector.tensor_tensor(smallest[:], low[:, :, 0], low[:, :, 1], ALU.min)
                uncombined = (c, group, largest, smallest)
        for c in ROUNDED_LATE:
            round_and_interleave(y_rounded[c][:], y[c][:], nc.scalar.copy)
            store_codes(c)
        last = len(chunks) - 1
        combine(*uncombined)
        round_and_interleave(y_rounded[last][:], y[last][:])
        store_codes(last)
        for q in range(QUADRANTS):
            queue = nc.sync if q % 2 == 0 else nc.scalar
            queue.dma_start(out_2[0, 4 * q : 4 * q + 4, :].bitcast(I32), y_scales[32 * q : 32 * q + 4, :].bitcast(I32))
